import numpy as np
import ml_dtypes


def mxq(x, axis, fmt="e4m3"):
    dtype, down = {"e4m3": (ml_dtypes.float8_e4m3fn, 7), "e5m2": (ml_dtypes.float8_e5m2, 14)}[fmt]
    v = np.moveaxis(np.asarray(x, np.float32).astype(ml_dtypes.bfloat16).astype(np.float64), axis, -1)
    blocks = v.reshape(v.shape[:-1] + (-1, 32))
    amax = np.abs(blocks).max(-1, keepdims=True)
    byte = np.maximum(np.where(amax > 0, np.frexp(amax)[1] - 1 + 127, 0) - down, 1)
    scale = np.exp2(byte - 127.0)
    codes = (blocks / scale).astype(np.float32).astype(dtype).astype(np.float64)
    return np.moveaxis((codes * scale).reshape(v.shape), -1, axis)


WIDE = False


def mx_kscale(k):
    if not WIDE:
        return np.ones(k)
    levels = np.array([10, -10, 5, -5, 0])
    if k % 512:
        return np.exp2(np.random.permutation(np.resize(levels, k // 32))).repeat(32)
    a = np.empty((k // 512, 16))
    for p in range(k // 512):
        a[p, :8] = np.random.permutation(np.resize(levels, 8))
        for g in range(8):
            far = levels[np.abs(levels - a[p, g]) >= 10]
            a[p, g + 8] = far[np.random.randint(len(far))]
    return np.exp2(a.ravel()).repeat(32)


def f64(x):
    return np.asarray(x).astype(np.float64)


def striped(idx):
    return np.tile(idx.reshape(-1, 16).T, (8, 1)).astype(np.uint16)


def unstriped(offs):
    return offs[:16].T.reshape(-1).astype(np.int64)


def pack_weight(w):
    k, n = w.shape
    w = f64(np.asarray(w, np.float32).astype(ml_dtypes.bfloat16)).reshape(k // 32, 32, n)
    amax = np.abs(w).max(1)
    byte = np.clip(np.where(amax > 0, np.frexp(amax)[1] - 1 + 127 - 7, 1), 1, 254)
    scaled = (w * np.exp2(127.0 - byte)[:, None, :]).reshape(k, n).astype(np.float32)
    words = np.ascontiguousarray(scaled.reshape(k // 512, 128, 4, n).transpose(0, 1, 3, 2)).astype(ml_dtypes.float8_e4m3fn).view(np.uint8)
    return words, np.ascontiguousarray(byte.astype(np.uint8).reshape(k // 512, 16, n))


def unpack_weight(words, scales):
    g, p, n, _ = words.shape
    vals = np.ascontiguousarray(words).view(ml_dtypes.float8_e4m3fn).astype(np.float64) * np.repeat(np.exp2(scales.astype(np.float64) - 127.0), 8, axis=1)[..., None]
    return vals.transpose(0, 1, 3, 2).reshape(g * 512, n)


E2M1 = np.array([0.0, 0.5, 1.0, 1.5, 2.0, 3.0, 4.0, 6.0, -0.0, -0.5, -1.0, -1.5, -2.0, -3.0, -4.0, -6.0])


def pack_fp4(w):
    k, n = w.shape
    w = f64(np.asarray(w, np.float32).astype(ml_dtypes.bfloat16)).reshape(k // 32, 32, n)
    amax = np.abs(w).max(1)
    mant, ex = np.frexp(amax / 6.0)
    byte = np.clip(np.where(amax > 0, np.where(mant > 0.5, ex, ex - 1) + 127, 1), 1, 254)
    scaled = (w * np.exp2(127.0 - byte)[:, None, :]).reshape(k, n).astype(np.float32)
    c = np.ascontiguousarray(scaled.reshape(k // 512, 128, 4, n).transpose(0, 1, 3, 2)).astype(ml_dtypes.float4_e2m1fn).view(np.uint8) & 0xF
    words = (c[..., 0::2] | (c[..., 1::2] << 4)).reshape(k // 512, 128, 2 * n)
    return np.ascontiguousarray(words), np.ascontiguousarray(byte.astype(np.uint8).reshape(k // 512, 16, n))


def unpack_fp4(words, scales):
    g, _, n = scales.shape
    words = np.ascontiguousarray(words).reshape(g, 128, n, 2)
    nib = np.empty((g, 128, n, 4), np.uint8)
    nib[..., 0::2] = words & 0xF
    nib[..., 1::2] = words >> 4
    vals = E2M1[nib] * np.repeat(np.exp2(scales.astype(np.float64) - 127.0), 8, axis=1)[..., None]
    return vals.transpose(0, 1, 3, 2).reshape(g * 512, n)


K, T, S, D, N, H, V, U = 1024, 2048, 1024, 4, 128, 512, 256, 512


def setup_inputs():
    n = np.random.standard_normal
    s = mx_kscale(K)[:, None]
    u = mx_kscale(H)
    packed_xT = pack_weight(n((K, T)) * s)
    packed_w1 = pack_fp4(n((K, H)) / np.sqrt(K) / s)
    packed_w2 = pack_fp4(n((H, N)) / np.sqrt(H) / u[:, None])
    return {
        "x_words": packed_xT[0],
        "x_scales": packed_xT[1],
        "w1_words": packed_w1[0],
        "w1_scales": packed_w1[1],
        "tri": (np.random.uniform(0.05, 0.6, (H, S))).astype(np.float32),
        "lod": (np.random.uniform(0.2, 1.0, (H, U))).astype(np.float32),
        "unit": (np.random.uniform(0.6, 1.4, (H, 1)) * u[:, None]).astype(np.float32),
        "w2_words": packed_w2[0],
        "w2_scales": packed_w2[1],
        "offs": striped(np.random.permutation(T)[:S]),
        "smp": striped(np.random.permutation(np.concatenate([np.arange(V), np.random.randint(0, V, U - V)]))),
    }


def reference(x_words, x_scales, w1_words, w1_scales, tri, lod, unit, w2_words, w2_scales, offs, smp):
    xq = unpack_weight(x_words, x_scales)[:, unstriped(offs)]
    y = unpack_fp4(w1_words, w1_scales).T @ xq
    yw = y * f64(tri)
    feat = yw.reshape(len(yw), -1, D).sum(axis=2)
    fs = feat[:, unstriped(smp)]
    fm = fs * f64(lod)
    rng_ = y.reshape(len(y), -1, D).max(axis=2) - (y.reshape(len(y), -1, D).min(axis=2))
    gs = rng_[:, unstriped(smp)]
    hid = f64(unit) * (fm - (0.5 * (gs * (-1.0 * f64(lod) + 1.0))))
    return unpack_fp4(w2_words, w2_scales).T @ mxq(hid, 0, "e4m3")

@@ -1,0 +1,231 @@
+from contextlib import ExitStack
+
+import concourse.mybir as mybir
+from concourse.masks import make_identity
+
+K, T, S, D, N, H, V, U = 1024, 2048, 1024, 4, 128, 512, 256, 512
+FLOPS = 2 * K * H * S + 2 * H * N * U
+
+F32 = mybir.dt.float32
+BF16 = mybir.dt.bfloat16
+I32 = mybir.dt.int32
+U32 = mybir.dt.uint32
+U16 = mybir.dt.uint16
+U8 = mybir.dt.uint8
+FP8X4 = mybir.dt.float8_e4m3fn_x4
+FP4X4 = mybir.dt.float4_e2m1fn_x4
+ALU = mybir.AluOpType
+COPY = mybir.ActivationFunctionType.Copy
+
+P = 128
+PASSES = 2
+TILES = 4
+HALF = 512
+CELLS = 128
+DEAL = "v16"
+RANGE_ON_GPSIMD = (0, 1, 2)
+
+
+def tile_picked_yhashf_fade_p_kernel(
+    tc, x_words, x_scales, w1_words, w1_scales, tri, lod, unit, w2_words, w2_scales, offs, smp, out
+):
+    nc = tc.nc
+    with ExitStack() as ctx:
+        keep = ctx.enter_context(tc.tile_pool(name="keep", bufs=1))
+        psum = ctx.enter_context(tc.psum_pool(name="psum", bufs=1))
+
+        offs_t = keep.tile([P, S // 16], U16, name="offs_t")
+        smp_t = keep.tile([P, U // 16], U16, name="smp_t")
+        xw = [keep.tile([P, T], U32, name=f"xw{g}", align_bytes=64) for g in range(PASSES)]
+        xs = keep.tile([P, T], U8, name="xs", align_bytes=64)
+        w1raw = keep.tile([P, PASSES, 2 * H], U8, name="w1raw", align_bytes=64)
+        w1sraw = keep.tile([P, PASSES, H], U8, name="w1sraw", align_bytes=64)
+        w1d = keep.tile([P, PASSES, TILES, 2 * P], U8, name="w1d", align_bytes=64)
+        w1sd = keep.tile([P, PASSES, TILES, P], U8, name="w1sd", align_bytes=64)
+        w2w = keep.tile([P, 2 * N], U8, name="w2w", align_bytes=64)
+        w2s = keep.tile([P, N], U8, name="w2s", align_bytes=64)
+        sg0 = keep.tile([P, S], U8, name="sg0", align_bytes=64)
+        sg = keep.tile([P, PASSES, S], U8, name="sg", align_bytes=64)
+        xg = [[keep.tile([P, HALF], U32, name=f"xg{g}{h}", align_bytes=64) for h in range(2)] for g in range(PASSES)]
+        tri_t = [keep.tile([P, S], F32, name=f"tri{t}", align_bytes=64) for t in range(TILES)]
+        lod_t = [keep.tile([P, U], F32, name=f"lod{t}", align_bytes=64) for t in range(TILES)]
+        unit_t = keep.tile([P, TILES], F32, name="unit_t")
+        neg_unit = keep.tile([P, TILES], F32, name="neg_unit")
+        ident = keep.tile([P, P], F32, name="ident", align_bytes=64)
+
+        nc.vector.memset(xs[32:64, :].bitcast(I32), 0)
+        nc.vector.memset(xs[64:128, :].bitcast(I32), 0)
+        nc.gpsimd.memset(w1sraw[:].rearrange("p g c -> p (g c)").bitcast(I32), 0)
+        nc.gpsimd.memset(sg[:].rearrange("p g c -> p (g c)").bitcast(I32), 0)
+        nc.gpsimd.memset(w2s[:].bitcast(I32), 0)
+        make_identity(nc, ident[:])
+
+        nc.sync.dma_start(xs[0:32, :].bitcast(I32), x_scales.rearrange("g q c -> q g c").bitcast(I32))
+        nc.sync.dma_start(offs_t[:], offs)
+        nc.sync.dma_start(w1raw[:].bitcast(I32), w1_words.rearrange("g p b -> p g b").bitcast(I32))
+        for q in range(4):
+            nc.sync.dma_start(
+                w1sraw[32 * q : 32 * q + 4].bitcast(I32),
+                w1_scales[:, 4 * q : 4 * q + 4, :].rearrange("g r c -> r g c").bitcast(I32),
+            )
+        for g in range(PASSES):
+            nc.sync.dma_start(xw[g][:].bitcast(I32), x_words[g].rearrange("p n t -> p (n t)").bitcast(I32))
+        nc.scalar.dma_start(unit_t[:], unit.rearrange("(p t) o -> p (t o)", t=TILES))
+        nc.scalar.activation(neg_unit[:], unit_t[:], COPY, scale=-1.0)
+        tri_rows = tri.rearrange("(p t) j -> t p j", t=TILES)
+        lod_rows = lod.rearrange("(p t) r -> t p r", t=TILES)
+        for t in range(TILES):
+            nc.sync.dma_start(tri_t[t][:], tri_rows[t])
+            if t == 0:
+                nc.sync.dma_start(smp_t[:], smp)
+        for t in range(TILES):
+            nc.sync.dma_start(lod_t[t][:], lod_rows[t])
+        nc.sync.dma_start(w2w[:].bitcast(I32), w2_words[0].bitcast(I32))
+        for q in range(4):
+            nc.sync.dma_start(w2s[32 * q : 32 * q + 4, :].bitcast(I32), w2_scales[0, 4 * q : 4 * q + 4, :].bitcast(I32))
+
+        nc.vector.tensor_copy(sg0[:], xs[:].indirect(offs_t[:]))
+        for q in range(4):
+            nc.scalar.dma_start(
+                sg[32 * q : 32 * q + 4].rearrange("p g c -> p (g c)").bitcast(I32), sg0[8 * q : 8 * q + 8, :].bitcast(I32)
+            )
+
+        def gather_words(g):
+            for h in range(2):
+                nc.vector.tensor_copy(xg[g][h][:], xw[g][:].indirect(offs_t[:, 32 * h : 32 * (h + 1)]))
+
+        if DEAL == "v16":
+            nc.vector.tensor_copy(
+                w1d[:].bitcast(U16), w1raw[:].bitcast(U16).rearrange("p g (m t) -> p g t m", t=TILES)
+            )
+            nc.vector.tensor_copy(w1sd[:], w1sraw[:].rearrange("p g (m t) -> p g t m", t=TILES))
+        elif DEAL == "v8":
+            nc.vector.tensor_copy(
+                w1d[:].rearrange("p g t (m b) -> p g t m b", b=2),
+                w1raw[:].rearrange("p g (m t b) -> p g t m b", t=TILES, b=2),
+            )
+            nc.vector.tensor_copy(w1sd[:], w1sraw[:].rearrange("p g (m t) -> p g t m", t=TILES))
+        else:
+            for g in range(PASSES):
+                nc.gpsimd.tensor_copy(
+                    w1d[:, g].rearrange("p t (m b) -> p t m b", b=2),
+                    w1raw[:, g].rearrange("p (m t b) -> p t m b", t=TILES, b=2),
+                )
+                nc.gpsimd.tensor_copy(w1sd[:, g], w1sraw[:, g].rearrange("p (m t) -> p t m", t=TILES))
+        gather_words(0)
+        gather_words(1)
+
+        def product_pass(bank, t, h, g):
+            nc.tensor.matmul_mx(
+                bank[:, HALF * h : HALF * (h + 1)],
+                lhsT=w1d[:, g, t, :].bitcast(FP4X4),
+                lhsT_scale=w1sd[:, g, t, :],
+                rhs=xg[g][h][:].bitcast(FP8X4),
+                rhs_scale=sg[:, g, HALF * h : HALF * (h + 1)],
+                start=(g == 0),
+                stop=(g == PASSES - 1),
+            )
+
+        y = {}
+        for t in range(3):
+            y[t] = psum.tile([P, S], F32, name=f"y{t}", tag=f"pair{t}")
+            for g in range(PASSES):
+                for h in range(2):
+                    product_pass(y[t], t, h, g)
+
+        hid = keep.tile([P, TILES, U], BF16, name="hid", align_bytes=64)
+        pw = [keep.tile([P, 3 * V], F32, name=f"pw{t}", align_bytes=64) for t in range(TILES)]
+        rw = [keep.tile([P, 4 * V], F32, name=f"rw{t}", align_bytes=64) for t in range(TILES)]
+        pg = [keep.tile([P, U], F32, name=f"pg{t}", align_bytes=64) for t in range(TILES)]
+        rg = [keep.tile([P, U], F32, name=f"rg{t}", align_bytes=64) for t in range(TILES)]
+
+        def corners(t):
+            yw = keep.tile([P, 2, V, 2], F32, name=f"yw{t}", align_bytes=64)
+            run = keep.tile([P, 2, 2, V], F32, name=f"run{t}", tag="scratch", align_bytes=64)
+            upper = pw[t][:, V : 3 * V].rearrange("p (e v) -> p e v", e=2)
+            yv = y[t][:].rearrange("p (v d) -> p d v", d=D)
+            for h in range(2):
+                cells = slice(CELLS * h, CELLS * (h + 1))
+                nc.scalar.activation(upper[:, :, cells], yv[:, 2:4, cells], COPY, scale=0.5)
+                nc.vector.tensor_tensor(
+                    yw[:, :, cells, :].rearrange("p k v e -> p v k e"),
+                    y[t][:].rearrange("p (v k e) -> p v k e", k=2, e=2)[:, cells],
+                    tri_t[t][:].rearrange("p (v k e) -> p v k e", k=2, e=2)[:, cells],
+                    ALU.mult,
+                )
+                for c, op in enumerate((ALU.max, ALU.min)):
+                    nc.vector.scalar_tensor_tensor(
+                        run[:, c, :, cells], yv[:, 0:2, cells], 0.5, upper[:, :, cells], ALU.mult, op
+                    )
+            for c, op in enumerate((ALU.max, ALU.min)):
+                nc.vector.tensor_tensor(rw[t][:, (1 + c) * V : (2 + c) * V], run[:, c, 0, :], run[:, c, 1, :], op)
+            eng = nc.gpsimd if t in RANGE_ON_GPSIMD else nc.vector
+            eng.tensor_tensor(rw[t][:, 0:V], rw[t][:, V : 2 * V], rw[t][:, 2 * V : 3 * V], ALU.subtract)
+            return yw
+
+        def tables(t, yw):
+            bank = psum.tile([P, HALF], F32, name=f"tp{t}", tag=f"bank{6 + t % 2}")
+            halves = [slice(CELLS * h, CELLS * (h + 1)) for h in range(2)]
+            terms = [(cells, yw[:, k, cells, e]) for cells in halves for k in range(2) for e in range(2)]
+            terms = terms + [(cells, rw[t][:, cells]) for cells in halves]
+            for i, (cells, term) in enumerate(terms):
+                nc.tensor.matmul(
+                    bank[:, cells], lhsT=term, rhs=ident[:], is_transpose=True,
+                    start=(i == 0), stop=(i == len(terms) - 1),
+                )
+            turned = rw[t][:, 3 * V : 4 * V]
+            nc.scalar.copy(turned, bank[:, 0:V])
+            for h in range(2):
+                cells = slice(CELLS * h, CELLS * (h + 1))
+                nc.tensor.transpose(bank[:, V + CELLS * h : V + CELLS * (h + 1)], turned[:, cells], ident[:])
+            nc.scalar.activation(rg[t][:], rw[t][:].indirect(smp_t[:]), COPY)
+            nc.scalar.activation(pw[t][:, 0:V], bank[:, V : 2 * V], COPY, scale=unit_t[:, t : t + 1])
+            parts = 2 if t == TILES - 1 else 1
+            for h in range(parts):
+                nc.scalar.activation(
+                    pg[t][:, U // parts * h : U // parts * (h + 1)],
+                    pw[t][:].indirect(smp_t[:, 32 // parts * h : 32 // parts * (h + 1)]),
+                    COPY,
+                )
+
+        def samples(faded, t, cols):
+            nc.vector.tensor_tensor(faded[:, t, cols], pg[t][:, cols], lod_t[t][:, cols], ALU.mult)
+            return lambda: nc.vector.scalar_tensor_tensor(
+                hid[:, t, cols], rg[t][:, cols], neg_unit[:, t : t + 1], faded[:, t, cols], ALU.mult, ALU.add
+            )
+
+        for t in range(TILES):
+            yw = corners(t)
+            if t == 0:
+                y[3] = psum.tile([P, S], F32, name="y3", tag="pair0")
+                for h in range(2):
+                    for g in range(PASSES):
+                        product_pass(y[3], 3, h, g)
+            tables(t, yw)
+        faded = keep.tile([P, TILES, U], F32, name="faded", tag="scratch", align_bytes=64)
+        finish = [samples(faded, t, slice(0, U)) for t in range(TILES - 1)]
+        for f in finish:
+            f()
+        finish = [samples(faded, TILES - 1, slice(V * h, V * (h + 1))) for h in range(2)]
+        for f in finish:
+            f()
+
+        woven = [keep.tile([P, V, TILES], BF16, name=f"woven{h}", align_bytes=64) for h in range(2)]
+        codes = [keep.tile([P, V], U32, name=f"codes{h}", align_bytes=64) for h in range(2)]
+        planes = [keep.tile([P, V], U8, name=f"planes{h}", align_bytes=64) for h in range(2)]
+        for h in range(2):
+            nc.vector.tensor_copy(
+                woven[h][:].rearrange("p (c i) t -> p c t i", i=4),
+                hid[:, :, V * h : V * (h + 1)].rearrange("p t (c i) -> p c t i", i=4),
+            )
+        for h in range(2):
+            nc.vector.quantize_mx(codes[h][:].bitcast(FP8X4), planes[h][:], woven[h][:].rearrange("p r t -> p (r t)"))
+        for h in range(2):
+            acc = psum.tile([P, V], F32, name=f"acc{h}", tag=f"bank{6 + h}")
+            nc.tensor.matmul_mx(
+                acc[:], lhsT=w2w[:].bitcast(FP4X4), lhsT_scale=w2s[:],
+                rhs=codes[h][:].bitcast(FP8X4), rhs_scale=planes[h][:], start=True, stop=True,
+            )
+            res = keep.tile([P, V], F32, name=f"res{h}", align_bytes=64)
+            nc.scalar.copy(res[:], acc[:])
+            nc.sync.dma_start(out[:, V * h : V * (h + 1)], res[:])

@@ -22,7 +22,6 @@ PASSES = 2
 TILES = 4
 HALF = 512
 CELLS = 128
-DEAL = "v16"
 RANGE_ON_GPSIMD = (0, 1, 2)
 
 
@@ -36,90 +35,90 @@ def tile_picked_yhashf_fade_p_kernel(
 
         offs_t = keep.tile([P, S // 16], U16, name="offs_t")
         smp_t = keep.tile([P, U // 16], U16, name="smp_t")
-        xw = [keep.tile([P, T], U32, name=f"xw{g}", align_bytes=64) for g in range(PASSES)]
-        xs = keep.tile([P, T], U8, name="xs", align_bytes=64)
-        w1raw = keep.tile([P, PASSES, 2 * H], U8, name="w1raw", align_bytes=64)
-        w1sraw = keep.tile([P, PASSES, H], U8, name="w1sraw", align_bytes=64)
-        w1d = keep.tile([P, PASSES, TILES, 2 * P], U8, name="w1d", align_bytes=64)
-        w1sd = keep.tile([P, PASSES, TILES, P], U8, name="w1sd", align_bytes=64)
-        w2w = keep.tile([P, 2 * N], U8, name="w2w", align_bytes=64)
-        w2s = keep.tile([P, N], U8, name="w2s", align_bytes=64)
-        sg0 = keep.tile([P, S], U8, name="sg0", align_bytes=64)
+        xw = [keep.tile([P, T], U32, name=f"xw{g}", tag=f"xw{g}", align_bytes=64) for g in range(PASSES)]
+        xs = keep.tile([P, T], U8, name="xs", tag="xs", align_bytes=64)
+        w1raw = keep.tile([P, PASSES, 2 * H], U8, name="w1raw", tag="w1raw", align_bytes=64)
+        w1sraw = keep.tile([P, PASSES, H], U8, name="w1sraw", tag="w1sraw", align_bytes=64)
+        early = keep.tile([P, 2 * PASSES * 3 * P], U8, name="early", align_bytes=64)
+        sg0 = keep.tile([P, S], U8, name="sg0", tag="sg0", align_bytes=64)
         sg = keep.tile([P, PASSES, S], U8, name="sg", align_bytes=64)
-        xg = [[keep.tile([P, HALF], U32, name=f"xg{g}{h}", align_bytes=64) for h in range(2)] for g in range(PASSES)]
-        tri_t = [keep.tile([P, S], F32, name=f"tri{t}", align_bytes=64) for t in range(TILES)]
-        lod_t = [keep.tile([P, U], F32, name=f"lod{t}", align_bytes=64) for t in range(TILES)]
-        unit_t = keep.tile([P, TILES], F32, name="unit_t")
+        xg = [[keep.tile([P, HALF], U32, name=f"xg{g}{h}", tag=f"xg{g}{h}", align_bytes=64) for h in range(2)] for g in range(PASSES)]
         neg_unit = keep.tile([P, TILES], F32, name="neg_unit")
         ident = keep.tile([P, P], F32, name="ident", align_bytes=64)
 
-        nc.vector.memset(xs[32:64, :].bitcast(I32), 0)
+        nc.vector.memset(w1sraw[:].rearrange("p g c -> p (g c)").bitcast(I32), 0)
         nc.vector.memset(xs[64:128, :].bitcast(I32), 0)
-        nc.gpsimd.memset(w1sraw[:].rearrange("p g c -> p (g c)").bitcast(I32), 0)
+        nc.gpsimd.memset(xs[32:64, :].bitcast(I32), 0)
         nc.gpsimd.memset(sg[:].rearrange("p g c -> p (g c)").bitcast(I32), 0)
-        nc.gpsimd.memset(w2s[:].bitcast(I32), 0)
         make_identity(nc, ident[:])
+
+        def load_words(g):
+            nc.sync.dma_start(xw[g][:].bitcast(I32), x_words[g].rearrange("p n t -> p (n t)").bitcast(I32))
 
         nc.sync.dma_start(xs[0:32, :].bitcast(I32), x_scales.rearrange("g q c -> q g c").bitcast(I32))
         nc.sync.dma_start(offs_t[:], offs)
+        nc.sync.dma_start(smp_t[:], smp)
         nc.sync.dma_start(w1raw[:].bitcast(I32), w1_words.rearrange("g p b -> p g b").bitcast(I32))
+        load_words(0)
         for q in range(4):
             nc.sync.dma_start(
                 w1sraw[32 * q : 32 * q + 4].bitcast(I32),
                 w1_scales[:, 4 * q : 4 * q + 4, :].rearrange("g r c -> r g c").bitcast(I32),
             )
-        for g in range(PASSES):
-            nc.sync.dma_start(xw[g][:].bitcast(I32), x_words[g].rearrange("p n t -> p (n t)").bitcast(I32))
-        nc.scalar.dma_start(unit_t[:], unit.rearrange("(p t) o -> p (t o)", t=TILES))
-        nc.scalar.activation(neg_unit[:], unit_t[:], COPY, scale=-1.0)
-        tri_rows = tri.rearrange("(p t) j -> t p j", t=TILES)
-        lod_rows = lod.rearrange("(p t) r -> t p r", t=TILES)
-        for t in range(TILES):
-            nc.sync.dma_start(tri_t[t][:], tri_rows[t])
-            if t == 0:
-                nc.sync.dma_start(smp_t[:], smp)
-        for t in range(TILES):
-            nc.sync.dma_start(lod_t[t][:], lod_rows[t])
-        nc.sync.dma_start(w2w[:].bitcast(I32), w2_words[0].bitcast(I32))
-        for q in range(4):
-            nc.sync.dma_start(w2s[32 * q : 32 * q + 4, :].bitcast(I32), w2_scales[0, 4 * q : 4 * q + 4, :].bitcast(I32))
+        load_words(1)
 
         nc.vector.tensor_copy(sg0[:], xs[:].indirect(offs_t[:]))
         for q in range(4):
-            nc.scalar.dma_start(
+            nc.sync.dma_start(
                 sg[32 * q : 32 * q + 4].rearrange("p g c -> p (g c)").bitcast(I32), sg0[8 * q : 8 * q + 8, :].bitcast(I32)
             )
 
-        def gather_words(g):
-            for h in range(2):
-                nc.vector.tensor_copy(xg[g][h][:], xw[g][:].indirect(offs_t[:, 32 * h : 32 * (h + 1)]))
+        def gather_words(g, h):
+            nc.vector.tensor_copy(xg[g][h][:], xw[g][:].indirect(offs_t[:, 32 * h : 32 * (h + 1)]))
 
-        if DEAL == "v16":
-            nc.vector.tensor_copy(
-                w1d[:].bitcast(U16), w1raw[:].bitcast(U16).rearrange("p g (m t) -> p g t m", t=TILES)
-            )
-            nc.vector.tensor_copy(w1sd[:], w1sraw[:].rearrange("p g (m t) -> p g t m", t=TILES))
-        elif DEAL == "v8":
-            nc.vector.tensor_copy(
-                w1d[:].rearrange("p g t (m b) -> p g t m b", b=2),
-                w1raw[:].rearrange("p g (m t b) -> p g t m b", t=TILES, b=2),
-            )
-            nc.vector.tensor_copy(w1sd[:], w1sraw[:].rearrange("p g (m t) -> p g t m", t=TILES))
-        else:
-            for g in range(PASSES):
-                nc.gpsimd.tensor_copy(
-                    w1d[:, g].rearrange("p t (m b) -> p t m b", b=2),
-                    w1raw[:, g].rearrange("p (m t b) -> p t m b", t=TILES, b=2),
-                )
-                nc.gpsimd.tensor_copy(w1sd[:, g], w1sraw[:, g].rearrange("p (m t) -> p t m", t=TILES))
-        gather_words(0)
-        gather_words(1)
+        def dealt_views(tile):
+            words = tile[:, 0 : 2 * PASSES * 2 * P].rearrange("p (t g b) -> p t g b", t=2, g=PASSES)
+            scales = tile[:, 2 * PASSES * 2 * P :].rearrange("p (t g m) -> p t g m", t=2, g=PASSES)
+            return words, scales
+
+        raw_scales = w1sraw[:].rearrange("p g (m t) -> p t g m", t=TILES)
+        words_lo, scales_lo = dealt_views(early)
+        nc.vector.tensor_copy(
+            words_lo.bitcast(U16), w1raw[:].bitcast(U16).rearrange("p g (m t) -> p t g m", t=TILES)[:, 0:2]
+        )
+        gather_words(0, 0)
+        nc.vector.tensor_copy(scales_lo, raw_scales[:, 0:2])
+        gather_words(0, 1)
+        gather_words(1, 0)
+        gather_words(1, 1)
+        late = keep.tile([P, 2 * PASSES * 3 * P], U8, name="late", tag="xw1", align_bytes=64)
+        words_hi, scales_hi = dealt_views(late)
+        raw_words = w1raw[:].rearrange("p g (m t b) -> p t g m b", t=TILES, b=2)
+        for t in range(2):
+            nc.gpsimd.tensor_copy(words_hi[:, t].rearrange("p g (m b) -> p g m b", b=2), raw_words[:, 2 + t])
+            nc.gpsimd.tensor_copy(scales_hi[:, t], raw_scales[:, 2 + t])
+        w1_codes = [words_lo[:, 0], words_lo[:, 1], words_hi[:, 0], words_hi[:, 1]]
+        w1_planes = [scales_lo[:, 0], scales_lo[:, 1], scales_hi[:, 0], scales_hi[:, 1]]
+
+        tri_rows = tri.rearrange("(p t) j -> p t j", t=TILES)
+        tri0 = keep.tile([P, S], F32, name="tri0", tag="xs", align_bytes=64)
+        nc.sync.dma_start(tri0[:], tri_rows[:, 0])
+        tri12 = keep.tile([P, 2, S], F32, name="tri12", tag="xw0", align_bytes=64)
+        for t in range(2):
+            nc.sync.dma_start(tri12[:, t], tri_rows[:, 1 + t])
+        tri3 = keep.tile([P, S + 16], F32, name="tri3", tag="sg0", align_bytes=64)
+        unit_t = tri3[:, S : S + TILES]
+        nc.sync.dma_start(unit_t, unit.rearrange("(p t) o -> p (t o)", t=TILES))
+        nc.sync.dma_start(tri3[:, 0:S], tri_rows[:, 3])
+        tri_t = [tri0[:], tri12[:, 0], tri12[:, 1], tri3[:, 0:S]]
+        lod_all = keep.tile([P, TILES, U], F32, name="lod_all", tag="w1raw", align_bytes=64)
+        nc.sync.dma_start(lod_all[:], lod.rearrange("(p t) r -> p t r", t=TILES))
 
         def product_pass(bank, t, h, g):
             nc.tensor.matmul_mx(
-                bank[:, HALF * h : HALF * (h + 1)],
-                lhsT=w1d[:, g, t, :].bitcast(FP4X4),
-                lhsT_scale=w1sd[:, g, t, :],
+                bank[:],
+                lhsT=w1_codes[t][:, g, :].bitcast(FP4X4),
+                lhsT_scale=w1_planes[t][:, g, :],
                 rhs=xg[g][h][:].bitcast(FP8X4),
                 rhs_scale=sg[:, g, HALF * h : HALF * (h + 1)],
                 start=(g == 0),
@@ -127,35 +126,47 @@ def tile_picked_yhashf_fade_p_kernel(
             )
 
         y = {}
-        for t in range(3):
-            y[t] = psum.tile([P, S], F32, name=f"y{t}", tag=f"pair{t}")
+        for t in range(TILES):
+            for h in range(2):
+                y[t, h] = psum.tile([P, HALF], F32, name=f"y{t}{h}", tag=f"bank{2 * t + h}")
             for g in range(PASSES):
                 for h in range(2):
-                    product_pass(y[t], t, h, g)
+                    product_pass(y[t, h], t, h, g)
+        w2w = keep.tile([P, 2 * N], U8, name="w2w", tag="xg00", align_bytes=64)
+        w2s = keep.tile([P, N], U8, name="w2s", tag="xg01", align_bytes=64)
+        nc.gpsimd.memset(w2s[:].bitcast(I32), 0)
+        nc.sync.dma_start(w2w[:].bitcast(I32), w2_words[0].bitcast(I32))
+        for q in range(4):
+            nc.sync.dma_start(w2s[32 * q : 32 * q + 4, :].bitcast(I32), w2_scales[0, 4 * q : 4 * q + 4, :].bitcast(I32))
 
         hid = keep.tile([P, TILES, U], BF16, name="hid", align_bytes=64)
-        pw = [keep.tile([P, 3 * V], F32, name=f"pw{t}", align_bytes=64) for t in range(TILES)]
-        rw = [keep.tile([P, 4 * V], F32, name=f"rw{t}", align_bytes=64) for t in range(TILES)]
-        pg = [keep.tile([P, U], F32, name=f"pg{t}", align_bytes=64) for t in range(TILES)]
+        pw = [keep.tile([P, (4 if t < 2 else 3) * V], F32, name=f"pw{t}", align_bytes=64) for t in range(TILES)]
+        own_turned = keep.tile([P, 2, V], F32, name="own_turned", align_bytes=64)
+        rw = [keep.tile([P, 3 * V], F32, name=f"rw{t}", align_bytes=64) for t in range(TILES)]
+        pg = {t: keep.tile([P, U], F32, name=f"pg{t}", align_bytes=64) for t in (0, 1, 3)}
         rg = [keep.tile([P, U], F32, name=f"rg{t}", align_bytes=64) for t in range(TILES)]
 
-        def corners(t):
-            yw = keep.tile([P, 2, V, 2], F32, name=f"yw{t}", align_bytes=64)
-            run = keep.tile([P, 2, 2, V], F32, name=f"run{t}", tag="scratch", align_bytes=64)
+        def copy_upper(t):
             upper = pw[t][:, V : 3 * V].rearrange("p (e v) -> p e v", e=2)
-            yv = y[t][:].rearrange("p (v d) -> p d v", d=D)
             for h in range(2):
                 cells = slice(CELLS * h, CELLS * (h + 1))
-                nc.scalar.activation(upper[:, :, cells], yv[:, 2:4, cells], COPY, scale=0.5)
+                nc.scalar.activation(upper[:, :, cells], y[t, h][:].rearrange("p (v d) -> p d v", d=D)[:, 2:4], COPY, scale=0.5)
+
+        def corners(t):
+            yw = keep.tile([P, 2, V, 2], F32, name=f"yw{t}", tag="yw", bufs=2, align_bytes=64)
+            run = keep.tile([P, 2, 2, V], F32, name=f"run{t}", tag="scratch", align_bytes=64)
+            upper = pw[t][:, V : 3 * V].rearrange("p (e v) -> p e v", e=2)
+            for h in range(2):
+                cells = slice(CELLS * h, CELLS * (h + 1))
                 nc.vector.tensor_tensor(
                     yw[:, :, cells, :].rearrange("p k v e -> p v k e"),
-                    y[t][:].rearrange("p (v k e) -> p v k e", k=2, e=2)[:, cells],
-                    tri_t[t][:].rearrange("p (v k e) -> p v k e", k=2, e=2)[:, cells],
+                    y[t, h][:].rearrange("p (v k e) -> p v k e", k=2, e=2),
+                    tri_t[t].rearrange("p (v k e) -> p v k e", k=2, e=2)[:, cells],
                     ALU.mult,
                 )
                 for c, op in enumerate((ALU.max, ALU.min)):
                     nc.vector.scalar_tensor_tensor(
-                        run[:, c, :, cells], yv[:, 0:2, cells], 0.5, upper[:, :, cells], ALU.mult, op
+                        run[:, c, :, cells], y[t, h][:].rearrange("p (v d) -> p d v", d=D)[:, 0:2], 0.5, upper[:, :, cells], ALU.mult, op
                     )
             for c, op in enumerate((ALU.max, ALU.min)):
                 nc.vector.tensor_tensor(rw[t][:, (1 + c) * V : (2 + c) * V], run[:, c, 0, :], run[:, c, 1, :], op)
@@ -164,7 +175,7 @@ def tile_picked_yhashf_fade_p_kernel(
             return yw
 
         def tables(t, yw):
-            bank = psum.tile([P, HALF], F32, name=f"tp{t}", tag=f"bank{6 + t % 2}")
+            bank = psum.tile([P, HALF], F32, name=f"tp{t}", tag=f"bank{2 * t}")
             halves = [slice(CELLS * h, CELLS * (h + 1)) for h in range(2)]
             terms = [(cells, yw[:, k, cells, e]) for cells in halves for k in range(2) for e in range(2)]
             terms = terms + [(cells, rw[t][:, cells]) for cells in halves]
@@ -173,13 +184,17 @@ def tile_picked_yhashf_fade_p_kernel(
                     bank[:, cells], lhsT=term, rhs=ident[:], is_transpose=True,
                     start=(i == 0), stop=(i == len(terms) - 1),
                 )
-            turned = rw[t][:, 3 * V : 4 * V]
+            turned = pw[t - 1][:, 3 * V : 4 * V] if t in (1, 2) else own_turned[:, t // 3, :]
+            nc.scalar.activation(rg[t][:], rw[t][:].indirect(smp_t[:]), COPY)
             nc.scalar.copy(turned, bank[:, 0:V])
             for h in range(2):
                 cells = slice(CELLS * h, CELLS * (h + 1))
                 nc.tensor.transpose(bank[:, V + CELLS * h : V + CELLS * (h + 1)], turned[:, cells], ident[:])
-            nc.scalar.activation(rg[t][:], rw[t][:].indirect(smp_t[:]), COPY)
+            if t in (1, 2):
+                fetch_sums(t - 1)
             nc.scalar.activation(pw[t][:, 0:V], bank[:, V : 2 * V], COPY, scale=unit_t[:, t : t + 1])
+
+        def fetch_sums(t):
             parts = 2 if t == TILES - 1 else 1
             for h in range(parts):
                 nc.scalar.activation(
@@ -189,23 +204,24 @@ def tile_picked_yhashf_fade_p_kernel(
                 )
 
         def samples(faded, t, cols):
-            nc.vector.tensor_tensor(faded[:, t, cols], pg[t][:, cols], lod_t[t][:, cols], ALU.mult)
+            sums = pw[t][:].indirect(smp_t[:]) if t == 2 else pg[t][:, cols]
+            nc.vector.tensor_tensor(faded[:, t, cols], sums, lod_all[:, t, cols], ALU.mult)
             return lambda: nc.vector.scalar_tensor_tensor(
                 hid[:, t, cols], rg[t][:, cols], neg_unit[:, t : t + 1], faded[:, t, cols], ALU.mult, ALU.add
             )
 
         for t in range(TILES):
+            copy_upper(t)
+        nc.scalar.activation(neg_unit[:], unit_t, COPY, scale=-1.0)
+        for t in range(TILES):
             yw = corners(t)
-            if t == 0:
-                y[3] = psum.tile([P, S], F32, name="y3", tag="pair0")
-                for h in range(2):
-                    for g in range(PASSES):
-                        product_pass(y[3], 3, h, g)
             tables(t, yw)
+        fetch_sums(TILES - 1)
         faded = keep.tile([P, TILES, U], F32, name="faded", tag="scratch", align_bytes=64)
-        finish = [samples(faded, t, slice(0, U)) for t in range(TILES - 1)]
+        finish = [samples(faded, t, slice(0, U)) for t in range(2)]
         for f in finish:
             f()
+        samples(faded, 2, slice(0, U))()
         finish = [samples(faded, TILES - 1, slice(V * h, V * (h + 1))) for h in range(2)]
         for f in finish:
             f()
@@ -221,7 +237,7 @@ def tile_picked_yhashf_fade_p_kernel(
         for h in range(2):
             nc.vector.quantize_mx(codes[h][:].bitcast(FP8X4), planes[h][:], woven[h][:].rearrange("p r t -> p (r t)"))
         for h in range(2):
-            acc = psum.tile([P, V], F32, name=f"acc{h}", tag=f"bank{6 + h}")
+            acc = psum.tile([P, V], F32, name=f"acc{h}", tag=f"bank{1 + 2 * h}")
             nc.tensor.matmul_mx(
                 acc[:], lhsT=w2w[:].bitcast(FP4X4), lhsT_scale=w2s[:],
                 rhs=codes[h][:].bitcast(FP8X4), rhs_scale=planes[h][:], start=True, stop=True,

@@ -57,7 +57,6 @@ def tile_picked_yhashf_fade_p_kernel(
 
         nc.sync.dma_start(xs[0:32, :].bitcast(I32), x_scales.rearrange("g q c -> q g c").bitcast(I32))
         nc.sync.dma_start(offs_t[:], offs)
-        nc.sync.dma_start(smp_t[:], smp)
         nc.sync.dma_start(w1raw[:].bitcast(I32), w1_words.rearrange("g p b -> p g b").bitcast(I32))
         load_words(0)
         for q in range(4):
@@ -66,6 +65,7 @@ def tile_picked_yhashf_fade_p_kernel(
                 w1_scales[:, 4 * q : 4 * q + 4, :].rearrange("g r c -> r g c").bitcast(I32),
             )
         load_words(1)
+        nc.sync.dma_start(smp_t[:], smp)
 
         nc.vector.tensor_copy(sg0[:], xs[:].indirect(offs_t[:]))
         for q in range(4):
@@ -87,18 +87,20 @@ def tile_picked_yhashf_fade_p_kernel(
             words_lo.bitcast(U16), w1raw[:].bitcast(U16).rearrange("p g (m t) -> p t g m", t=TILES)[:, 0:2]
         )
         gather_words(0, 0)
-        nc.vector.tensor_copy(scales_lo, raw_scales[:, 0:2])
+        nc.vector.tensor_copy(scales_lo[:, 0], raw_scales[:, 0])
         gather_words(0, 1)
         gather_words(1, 0)
         gather_words(1, 1)
-        late = keep.tile([P, 2 * PASSES * 3 * P], U8, name="late", tag="xw1", align_bytes=64)
-        words_hi, scales_hi = dealt_views(late)
+        late = keep.tile([P, 2 * PASSES * 3 * P + PASSES * P], U8, name="late", tag="xw1", align_bytes=64)
+        words_hi, scales_hi = dealt_views(late[:, 0 : 2 * PASSES * 3 * P])
+        scales_one = late[:, 2 * PASSES * 3 * P :].rearrange("p (g m) -> p g m", g=PASSES)
+        nc.vector.tensor_copy(scales_one, raw_scales[:, 1])
         raw_words = w1raw[:].rearrange("p g (m t b) -> p t g m b", t=TILES, b=2)
         for t in range(2):
             nc.gpsimd.tensor_copy(words_hi[:, t].rearrange("p g (m b) -> p g m b", b=2), raw_words[:, 2 + t])
             nc.gpsimd.tensor_copy(scales_hi[:, t], raw_scales[:, 2 + t])
         w1_codes = [words_lo[:, 0], words_lo[:, 1], words_hi[:, 0], words_hi[:, 1]]
-        w1_planes = [scales_lo[:, 0], scales_lo[:, 1], scales_hi[:, 0], scales_hi[:, 1]]
+        w1_planes = [scales_lo[:, 0], scales_one, scales_hi[:, 0], scales_hi[:, 1]]
 
         tri_rows = tri.rearrange("(p t) j -> p t j", t=TILES)
         tri0 = keep.tile([P, S], F32, name="tri0", tag="xs", align_bytes=64)
@@ -129,8 +131,7 @@ def tile_picked_yhashf_fade_p_kernel(
         for t in range(TILES):
             for h in range(2):
                 y[t, h] = psum.tile([P, HALF], F32, name=f"y{t}{h}", tag=f"bank{2 * t + h}")
-            for g in range(PASSES):
-                for h in range(2):
+                for g in range(PASSES):
                     product_pass(y[t, h], t, h, g)
         w2w = keep.tile([P, 2 * N], U8, name="w2w", tag="xg00", align_bytes=64)
         w2s = keep.tile([P, N], U8, name="w2s", tag="xg01", align_bytes=64)
@@ -141,29 +142,31 @@ def tile_picked_yhashf_fade_p_kernel(
 
         hid = keep.tile([P, TILES, U], BF16, name="hid", align_bytes=64)
         pw = [keep.tile([P, (4 if t < 2 else 3) * V], F32, name=f"pw{t}", align_bytes=64) for t in range(TILES)]
-        own_turned = keep.tile([P, 2, V], F32, name="own_turned", align_bytes=64)
-        rw = [keep.tile([P, 3 * V], F32, name=f"rw{t}", align_bytes=64) for t in range(TILES)]
+        first_turned = keep.tile([P, V], F32, name="first_turned", align_bytes=64)
+        rw = [keep.tile([P, (4 if t == 3 else 3) * V], F32, name=f"rw{t}", align_bytes=64) for t in range(TILES)]
         pg = {t: keep.tile([P, U], F32, name=f"pg{t}", align_bytes=64) for t in (0, 1, 3)}
         rg = [keep.tile([P, U], F32, name=f"rg{t}", align_bytes=64) for t in range(TILES)]
 
-        def copy_upper(t):
+        def copy_upper(t, h):
             upper = pw[t][:, V : 3 * V].rearrange("p (e v) -> p e v", e=2)
-            for h in range(2):
-                cells = slice(CELLS * h, CELLS * (h + 1))
-                nc.scalar.activation(upper[:, :, cells], y[t, h][:].rearrange("p (v d) -> p d v", d=D)[:, 2:4], COPY, scale=0.5)
+            cells = slice(CELLS * h, CELLS * (h + 1))
+            nc.scalar.activation(upper[:, :, cells], y[t, h][:].rearrange("p (v d) -> p d v", d=D)[:, 2:4], COPY, scale=0.5)
 
-        def corners(t):
-            yw = keep.tile([P, 2, V, 2], F32, name=f"yw{t}", tag="yw", bufs=2, align_bytes=64)
+        def weigh(yw, t, h):
+            cells = slice(CELLS * h, CELLS * (h + 1))
+            nc.vector.tensor_tensor(
+                yw[:, :, cells, :].rearrange("p k v e -> p v k e"),
+                y[t, h][:].rearrange("p (v k e) -> p v k e", k=2, e=2),
+                tri_t[t].rearrange("p (v k e) -> p v k e", k=2, e=2)[:, cells],
+                ALU.mult,
+            )
+
+        def corners(t, yw):
             run = keep.tile([P, 2, 2, V], F32, name=f"run{t}", tag="scratch", align_bytes=64)
             upper = pw[t][:, V : 3 * V].rearrange("p (e v) -> p e v", e=2)
             for h in range(2):
                 cells = slice(CELLS * h, CELLS * (h + 1))
-                nc.vector.tensor_tensor(
-                    yw[:, :, cells, :].rearrange("p k v e -> p v k e"),
-                    y[t, h][:].rearrange("p (v k e) -> p v k e", k=2, e=2),
-                    tri_t[t].rearrange("p (v k e) -> p v k e", k=2, e=2)[:, cells],
-                    ALU.mult,
-                )
+                weigh(yw, t, h)
                 for c, op in enumerate((ALU.max, ALU.min)):
                     nc.vector.scalar_tensor_tensor(
                         run[:, c, :, cells], y[t, h][:].rearrange("p (v d) -> p d v", d=D)[:, 0:2], 0.5, upper[:, :, cells], ALU.mult, op
@@ -172,7 +175,6 @@ def tile_picked_yhashf_fade_p_kernel(
                 nc.vector.tensor_tensor(rw[t][:, (1 + c) * V : (2 + c) * V], run[:, c, 0, :], run[:, c, 1, :], op)
             eng = nc.gpsimd if t in RANGE_ON_GPSIMD else nc.vector
             eng.tensor_tensor(rw[t][:, 0:V], rw[t][:, V : 2 * V], rw[t][:, 2 * V : 3 * V], ALU.subtract)
-            return yw
 
         def tables(t, yw):
             bank = psum.tile([P, HALF], F32, name=f"tp{t}", tag=f"bank{2 * t}")
@@ -184,14 +186,17 @@ def tile_picked_yhashf_fade_p_kernel(
                     bank[:, cells], lhsT=term, rhs=ident[:], is_transpose=True,
                     start=(i == 0), stop=(i == len(terms) - 1),
                 )
-            turned = pw[t - 1][:, 3 * V : 4 * V] if t in (1, 2) else own_turned[:, t // 3, :]
-            nc.scalar.activation(rg[t][:], rw[t][:].indirect(smp_t[:]), COPY)
+            turned = [first_turned[:], pw[0][:, 3 * V :], pw[1][:, 3 * V :], rw[3][:, 3 * V :]][t]
+            if t < 3:
+                nc.scalar.activation(rg[t][:], rw[t][:].indirect(smp_t[:]), COPY)
             nc.scalar.copy(turned, bank[:, 0:V])
             for h in range(2):
                 cells = slice(CELLS * h, CELLS * (h + 1))
                 nc.tensor.transpose(bank[:, V + CELLS * h : V + CELLS * (h + 1)], turned[:, cells], ident[:])
             if t in (1, 2):
                 fetch_sums(t - 1)
+            if t == 3:
+                nc.scalar.activation(rg[t][:], rw[t][:].indirect(smp_t[:]), COPY)
             nc.scalar.activation(pw[t][:, 0:V], bank[:, V : 2 * V], COPY, scale=unit_t[:, t : t + 1])
 
         def fetch_sums(t):
@@ -210,33 +215,39 @@ def tile_picked_yhashf_fade_p_kernel(
                 hid[:, t, cols], rg[t][:, cols], neg_unit[:, t : t + 1], faded[:, t, cols], ALU.mult, ALU.add
             )
 
-        for t in range(TILES):
-            copy_upper(t)
+        for t in range(TILES - 1):
+            for h in range(2):
+                copy_upper(t, h)
         nc.scalar.activation(neg_unit[:], unit_t, COPY, scale=-1.0)
         for t in range(TILES):
-            yw = corners(t)
+            yw = keep.tile([P, 2, V, 2], F32, name=f"yw{t}", tag="yw", bufs=2, align_bytes=64)
+            corners(t, yw)
             tables(t, yw)
+            if t == 0:
+                for h in range(2):
+                    copy_upper(TILES - 1, h)
         fetch_sums(TILES - 1)
         faded = keep.tile([P, TILES, U], F32, name="faded", tag="scratch", align_bytes=64)
-        finish = [samples(faded, t, slice(0, U)) for t in range(2)]
+        samples(faded, 0, slice(0, U))()
+        finish = [samples(faded, t, slice(0, U)) for t in (1, 2)]
         for f in finish:
             f()
-        samples(faded, 2, slice(0, U))()
-        finish = [samples(faded, TILES - 1, slice(V * h, V * (h + 1))) for h in range(2)]
+        finish = [samples(faded, 3, slice(V * h, V * (h + 1))) for h in range(2)]
         for f in finish:
             f()
 
         woven = [keep.tile([P, V, TILES], BF16, name=f"woven{h}", align_bytes=64) for h in range(2)]
         codes = [keep.tile([P, V], U32, name=f"codes{h}", align_bytes=64) for h in range(2)]
         planes = [keep.tile([P, V], U8, name=f"planes{h}", align_bytes=64) for h in range(2)]
-        for h in range(2):
-            nc.vector.tensor_copy(
-                woven[h][:].rearrange("p (c i) t -> p c t i", i=4),
-                hid[:, :, V * h : V * (h + 1)].rearrange("p t (c i) -> p c t i", i=4),
+
+        def weave(copy, h, first, last):
+            copy(
+                woven[h][:, first:last].rearrange("p (c i) t -> p c t i", i=4),
+                hid[:, :, V * h + first : V * h + last].rearrange("p t (c i) -> p c t i", i=4),
             )
-        for h in range(2):
+
+        def decode(h):
             nc.vector.quantize_mx(codes[h][:].bitcast(FP8X4), planes[h][:], woven[h][:].rearrange("p r t -> p (r t)"))
-        for h in range(2):
             acc = psum.tile([P, V], F32, name=f"acc{h}", tag=f"bank{1 + 2 * h}")
             nc.tensor.matmul_mx(
                 acc[:], lhsT=w2w[:].bitcast(FP4X4), lhsT_scale=w2s[:],
@@ -244,4 +255,10 @@ def tile_picked_yhashf_fade_p_kernel(
             )
             res = keep.tile([P, V], F32, name=f"res{h}", align_bytes=64)
             nc.scalar.copy(res[:], acc[:])
-            nc.sync.dma_start(out[:, V * h : V * (h + 1)], res[:])
+            nc.scalar.dma_start(out[:, V * h : V * (h + 1)], res[:])
+
+        weave(nc.scalar.copy, 0, 0, V // 2)
+        weave(nc.vector.tensor_copy, 0, V // 2, V)
+        weave(nc.vector.tensor_copy, 1, 0, V)
+        decode(0)
+        decode(1)

@@ -22,7 +22,7 @@ PASSES = 2
 TILES = 4
 HALF = 512
 CELLS = 128
-RANGE_ON_GPSIMD = (0, 1, 2)
+RANGE_ON_GPSIMD = (1, 2)
 
 
 def tile_picked_yhashf_fade_p_kernel(
@@ -141,10 +141,10 @@ def tile_picked_yhashf_fade_p_kernel(
             nc.sync.dma_start(w2s[32 * q : 32 * q + 4, :].bitcast(I32), w2_scales[0, 4 * q : 4 * q + 4, :].bitcast(I32))
 
         hid = keep.tile([P, TILES, U], BF16, name="hid", align_bytes=64)
-        pw = [keep.tile([P, (4 if t < 2 else 3) * V], F32, name=f"pw{t}", align_bytes=64) for t in range(TILES)]
-        first_turned = keep.tile([P, V], F32, name="first_turned", align_bytes=64)
-        rw = [keep.tile([P, (4 if t == 3 else 3) * V], F32, name=f"rw{t}", align_bytes=64) for t in range(TILES)]
-        pg = {t: keep.tile([P, U], F32, name=f"pg{t}", align_bytes=64) for t in (0, 1, 3)}
+        pw = [keep.tile([P, 3 * V], F32, name=f"pw{t}", align_bytes=64) for t in range(TILES - 1)]
+        first_turned = keep.tile([P, V], F32, name="first_turned", tag="first_turned", align_bytes=64)
+        rw = [keep.tile([P, (4 if t > 0 else 3) * V], F32, name=f"rw{t}", align_bytes=64) for t in range(TILES)]
+        pg = [keep.tile([P, V if t == 2 else U], F32, name=f"pg{t}", align_bytes=64) for t in range(TILES)]
         rg = [keep.tile([P, U], F32, name=f"rg{t}", align_bytes=64) for t in range(TILES)]
 
         def copy_upper(t, h):
@@ -186,33 +186,27 @@ def tile_picked_yhashf_fade_p_kernel(
                     bank[:, cells], lhsT=term, rhs=ident[:], is_transpose=True,
                     start=(i == 0), stop=(i == len(terms) - 1),
                 )
-            turned = [first_turned[:], pw[0][:, 3 * V :], pw[1][:, 3 * V :], rw[3][:, 3 * V :]][t]
-            if t < 3:
-                nc.scalar.activation(rg[t][:], rw[t][:].indirect(smp_t[:]), COPY)
+            turned = rw[t][:, 3 * V :] if t > 0 else first_turned[:]
             nc.scalar.copy(turned, bank[:, 0:V])
             for h in range(2):
                 cells = slice(CELLS * h, CELLS * (h + 1))
                 nc.tensor.transpose(bank[:, V + CELLS * h : V + CELLS * (h + 1)], turned[:, cells], ident[:])
-            if t in (1, 2):
-                fetch_sums(t - 1)
-            if t == 3:
-                nc.scalar.activation(rg[t][:], rw[t][:].indirect(smp_t[:]), COPY)
+            nc.scalar.activation(rg[t][:], rw[t][:].indirect(smp_t[:]), COPY)
             nc.scalar.activation(pw[t][:, 0:V], bank[:, V : 2 * V], COPY, scale=unit_t[:, t : t + 1])
+            if t == 0:
+                pw.append(keep.tile([P, 3 * V], F32, name="pw3", tag="first_turned", align_bytes=64))
+                for h in range(2):
+                    copy_upper(TILES - 1, h)
+            for first, last in ([(0, U)], [(0, U)], [(0, V)], [(0, V), (V, U)])[t]:
+                nc.scalar.activation(pg[t][:, first:last], pw[t][:].indirect(smp_t[:, first // 16 : last // 16]), COPY)
 
-        def fetch_sums(t):
-            parts = 2 if t == TILES - 1 else 1
-            for h in range(parts):
-                nc.scalar.activation(
-                    pg[t][:, U // parts * h : U // parts * (h + 1)],
-                    pw[t][:].indirect(smp_t[:, 32 // parts * h : 32 // parts * (h + 1)]),
-                    COPY,
-                )
+        def fade(faded, t, first, last):
+            sums = pw[t][:].indirect(smp_t[:, first // 16 : last // 16]) if (t, first) == (2, V) else pg[t][:, first:last]
+            nc.vector.tensor_tensor(faded[:, t, first:last], sums, lod_all[:, t, first:last], ALU.mult)
 
-        def samples(faded, t, cols):
-            sums = pw[t][:].indirect(smp_t[:]) if t == 2 else pg[t][:, cols]
-            nc.vector.tensor_tensor(faded[:, t, cols], sums, lod_all[:, t, cols], ALU.mult)
-            return lambda: nc.vector.scalar_tensor_tensor(
-                hid[:, t, cols], rg[t][:, cols], neg_unit[:, t : t + 1], faded[:, t, cols], ALU.mult, ALU.add
+        def finish(faded, t, first, last):
+            nc.vector.scalar_tensor_tensor(
+                hid[:, t, first:last], rg[t][:, first:last], neg_unit[:, t : t + 1], faded[:, t, first:last], ALU.mult, ALU.add
             )
 
         for t in range(TILES - 1):
@@ -223,18 +217,17 @@ def tile_picked_yhashf_fade_p_kernel(
             yw = keep.tile([P, 2, V, 2], F32, name=f"yw{t}", tag="yw", bufs=2, align_bytes=64)
             corners(t, yw)
             tables(t, yw)
-            if t == 0:
-                for h in range(2):
-                    copy_upper(TILES - 1, h)
-        fetch_sums(TILES - 1)
         faded = keep.tile([P, TILES, U], F32, name="faded", tag="scratch", align_bytes=64)
-        samples(faded, 0, slice(0, U))()
-        finish = [samples(faded, t, slice(0, U)) for t in (1, 2)]
-        for f in finish:
-            f()
-        finish = [samples(faded, 3, slice(V * h, V * (h + 1))) for h in range(2)]
-        for f in finish:
-            f()
+        fade(faded, 0, 0, U)
+        fade(faded, 1, 0, U)
+        fade(faded, 2, V, U)
+        finish(faded, 0, 0, U)
+        fade(faded, 2, 0, V)
+        finish(faded, 1, 0, U)
+        finish(faded, 2, 0, U)
+        for step in (fade, finish):
+            for h in range(2):
+                step(faded, 3, V * h, V * (h + 1))
 
         woven = [keep.tile([P, V, TILES], BF16, name=f"woven{h}", align_bytes=64) for h in range(2)]
         codes = [keep.tile([P, V], U32, name=f"codes{h}", align_bytes=64) for h in range(2)]

@@ -18,11 +18,16 @@ ALU = mybir.AluOpType
 COPY = mybir.ActivationFunctionType.Copy
 
 P = 128
-PASSES = 2
-TILES = 4
-HALF = 512
-CELLS = 128
-RANGE_ON_GPSIMD = (1, 2)
+PASSES = K // 512
+TILES = H // P
+LAST = TILES - 1
+FUSED = 2
+QUADS = 4
+BANK = 512
+CELLS = BANK // D
+PART = U // 2
+PER_COLUMN = 16
+PAD = 16
 
 
 def tile_picked_yhashf_fade_p_kernel(
@@ -33,74 +38,79 @@ def tile_picked_yhashf_fade_p_kernel(
         keep = ctx.enter_context(tc.tile_pool(name="keep", bufs=1))
         psum = ctx.enter_context(tc.psum_pool(name="psum", bufs=1))
 
-        offs_t = keep.tile([P, S // 16], U16, name="offs_t")
-        smp_t = keep.tile([P, U // 16], U16, name="smp_t")
-        xw = [keep.tile([P, T], U32, name=f"xw{g}", tag=f"xw{g}", align_bytes=64) for g in range(PASSES)]
-        xs = keep.tile([P, T], U8, name="xs", tag="xs", align_bytes=64)
-        w1raw = keep.tile([P, PASSES, 2 * H], U8, name="w1raw", tag="w1raw", align_bytes=64)
-        w1sraw = keep.tile([P, PASSES, H], U8, name="w1sraw", tag="w1sraw", align_bytes=64)
+        offs_t = keep.tile([P, S // PER_COLUMN], U16, name="offs_t")
+        smp_t = keep.tile([P, U // PER_COLUMN], U16, name="smp_t")
+        x_table = [keep.tile([P, T], U32, name=f"xw{g}", tag=f"xw{g}", align_bytes=64) for g in range(PASSES)]
+        scale_table = keep.tile([P, T], U8, name="xs", tag="xs", align_bytes=64)
+        w1_raw = keep.tile([P, PASSES, 2 * H], U8, name="w1raw", tag="w1raw", align_bytes=64)
+        w1_raw_planes = keep.tile([P, PASSES, H], U8, name="w1sraw", tag="w1sraw", align_bytes=64)
         early = keep.tile([P, 2 * PASSES * 3 * P], U8, name="early", align_bytes=64)
-        sg0 = keep.tile([P, S], U8, name="sg0", tag="sg0", align_bytes=64)
-        sg = keep.tile([P, PASSES, S], U8, name="sg", align_bytes=64)
-        xg = [[keep.tile([P, HALF], U32, name=f"xg{g}{h}", tag=f"xg{g}{h}", align_bytes=64) for h in range(2)] for g in range(PASSES)]
+        picked_rows = keep.tile([P, S], U8, name="sg0", tag="sg0", align_bytes=64)
+        x_planes = keep.tile([P, PASSES, S], U8, name="sg", align_bytes=64)
+        x_codes = [
+            [keep.tile([P, BANK], U32, name=f"xg{g}{h}", tag=f"xg{g}{h}", align_bytes=64) for h in range(2)]
+            for g in range(PASSES)
+        ]
         neg_unit = keep.tile([P, TILES], F32, name="neg_unit")
         ident = keep.tile([P, P], F32, name="ident", align_bytes=64)
 
-        nc.vector.memset(w1sraw[:].rearrange("p g c -> p (g c)").bitcast(I32), 0)
-        nc.vector.memset(xs[64:128, :].bitcast(I32), 0)
-        nc.gpsimd.memset(xs[32:64, :].bitcast(I32), 0)
-        nc.gpsimd.memset(sg[:].rearrange("p g c -> p (g c)").bitcast(I32), 0)
+        nc.vector.memset(w1_raw_planes[:].rearrange("p g c -> p (g c)").bitcast(I32), 0)
+        nc.vector.memset(scale_table[64:128, :].bitcast(I32), 0)
+        nc.gpsimd.memset(scale_table[32:64, :].bitcast(I32), 0)
+        nc.gpsimd.memset(x_planes[:].rearrange("p g c -> p (g c)").bitcast(I32), 0)
         make_identity(nc, ident[:])
 
         def load_words(g):
-            nc.sync.dma_start(xw[g][:].bitcast(I32), x_words[g].rearrange("p n t -> p (n t)").bitcast(I32))
+            nc.sync.dma_start(x_table[g][:].bitcast(I32), x_words[g].rearrange("p n j -> p (n j)").bitcast(I32))
 
-        nc.sync.dma_start(xs[0:32, :].bitcast(I32), x_scales.rearrange("g q c -> q g c").bitcast(I32))
+        nc.sync.dma_start(scale_table[0:32, :].bitcast(I32), x_scales.rearrange("g q c -> q g c").bitcast(I32))
         nc.sync.dma_start(offs_t[:], offs)
-        nc.sync.dma_start(w1raw[:].bitcast(I32), w1_words.rearrange("g p b -> p g b").bitcast(I32))
+        nc.sync.dma_start(w1_raw[:].bitcast(I32), w1_words.rearrange("g p b -> p g b").bitcast(I32))
         load_words(0)
-        for q in range(4):
+        for q in range(QUADS):
             nc.sync.dma_start(
-                w1sraw[32 * q : 32 * q + 4].bitcast(I32),
+                w1_raw_planes[32 * q : 32 * q + 4].bitcast(I32),
                 w1_scales[:, 4 * q : 4 * q + 4, :].rearrange("g r c -> r g c").bitcast(I32),
             )
         load_words(1)
         nc.sync.dma_start(smp_t[:], smp)
 
-        nc.vector.tensor_copy(sg0[:], xs[:].indirect(offs_t[:]))
-        for q in range(4):
+        nc.vector.tensor_copy(picked_rows[:], scale_table[:].indirect(offs_t[:]))
+        for q in range(QUADS):
             nc.sync.dma_start(
-                sg[32 * q : 32 * q + 4].rearrange("p g c -> p (g c)").bitcast(I32), sg0[8 * q : 8 * q + 8, :].bitcast(I32)
+                x_planes[32 * q : 32 * q + 4].rearrange("p g c -> p (g c)").bitcast(I32),
+                picked_rows[8 * q : 8 * q + 8, :].bitcast(I32),
             )
 
         def gather_words(g, h):
-            nc.vector.tensor_copy(xg[g][h][:], xw[g][:].indirect(offs_t[:, 32 * h : 32 * (h + 1)]))
+            columns = BANK // PER_COLUMN
+            nc.vector.tensor_copy(x_codes[g][h][:], x_table[g][:].indirect(offs_t[:, columns * h : columns * (h + 1)]))
 
         def dealt_views(tile):
             words = tile[:, 0 : 2 * PASSES * 2 * P].rearrange("p (t g b) -> p t g b", t=2, g=PASSES)
             scales = tile[:, 2 * PASSES * 2 * P :].rearrange("p (t g m) -> p t g m", t=2, g=PASSES)
             return words, scales
 
-        raw_scales = w1sraw[:].rearrange("p g (m t) -> p t g m", t=TILES)
-        words_lo, scales_lo = dealt_views(early)
+        raw_scales = w1_raw_planes[:].rearrange("p g (m t) -> p t g m", t=TILES)
+        words_01, scales_01 = dealt_views(early)
         nc.vector.tensor_copy(
-            words_lo.bitcast(U16), w1raw[:].bitcast(U16).rearrange("p g (m t) -> p t g m", t=TILES)[:, 0:2]
+            words_01.bitcast(U16), w1_raw[:].bitcast(U16).rearrange("p g (m t) -> p t g m", t=TILES)[:, 0:2]
         )
         gather_words(0, 0)
-        nc.vector.tensor_copy(scales_lo[:, 0], raw_scales[:, 0])
+        nc.vector.tensor_copy(scales_01[:, 0], raw_scales[:, 0])
         gather_words(0, 1)
         gather_words(1, 0)
         gather_words(1, 1)
         late = keep.tile([P, 2 * PASSES * 3 * P + PASSES * P], U8, name="late", tag="xw1", align_bytes=64)
-        words_hi, scales_hi = dealt_views(late[:, 0 : 2 * PASSES * 3 * P])
-        scales_one = late[:, 2 * PASSES * 3 * P :].rearrange("p (g m) -> p g m", g=PASSES)
-        nc.vector.tensor_copy(scales_one, raw_scales[:, 1])
-        raw_words = w1raw[:].rearrange("p g (m t b) -> p t g m b", t=TILES, b=2)
+        words_23, scales_23 = dealt_views(late[:, 0 : 2 * PASSES * 3 * P])
+        scales_1 = late[:, 2 * PASSES * 3 * P :].rearrange("p (g m) -> p g m", g=PASSES)
+        nc.vector.tensor_copy(scales_1, raw_scales[:, 1])
+        raw_words = w1_raw[:].rearrange("p g (m t b) -> p t g m b", t=TILES, b=2)
         for t in range(2):
-            nc.gpsimd.tensor_copy(words_hi[:, t].rearrange("p g (m b) -> p g m b", b=2), raw_words[:, 2 + t])
-            nc.gpsimd.tensor_copy(scales_hi[:, t], raw_scales[:, 2 + t])
-        w1_codes = [words_lo[:, 0], words_lo[:, 1], words_hi[:, 0], words_hi[:, 1]]
-        w1_planes = [scales_lo[:, 0], scales_one, scales_hi[:, 0], scales_hi[:, 1]]
+            nc.gpsimd.tensor_copy(words_23[:, t].rearrange("p g (m b) -> p g m b", b=2), raw_words[:, 2 + t])
+            nc.gpsimd.tensor_copy(scales_23[:, t], raw_scales[:, 2 + t])
+        w1_codes = [words_01[:, 0], words_01[:, 1], words_23[:, 0], words_23[:, 1]]
+        w1_planes = [scales_01[:, 0], scales_1, scales_23[:, 0], scales_23[:, 1]]
 
         tri_rows = tri.rearrange("(p t) j -> p t j", t=TILES)
         tri0 = keep.tile([P, S], F32, name="tri0", tag="xs", align_bytes=64)
@@ -108,21 +118,21 @@ def tile_picked_yhashf_fade_p_kernel(
         tri12 = keep.tile([P, 2, S], F32, name="tri12", tag="xw0", align_bytes=64)
         for t in range(2):
             nc.sync.dma_start(tri12[:, t], tri_rows[:, 1 + t])
-        tri3 = keep.tile([P, S + 16], F32, name="tri3", tag="sg0", align_bytes=64)
-        unit_t = tri3[:, S : S + TILES]
+        tri3_unit = keep.tile([P, S + PAD], F32, name="tri3", tag="sg0", align_bytes=64)
+        unit_t = tri3_unit[:, S : S + TILES]
         nc.sync.dma_start(unit_t, unit.rearrange("(p t) o -> p (t o)", t=TILES))
-        nc.sync.dma_start(tri3[:, 0:S], tri_rows[:, 3])
-        tri_t = [tri0[:], tri12[:, 0], tri12[:, 1], tri3[:, 0:S]]
-        lod_all = keep.tile([P, TILES, U], F32, name="lod_all", tag="w1raw", align_bytes=64)
-        nc.sync.dma_start(lod_all[:], lod.rearrange("(p t) r -> p t r", t=TILES))
+        nc.sync.dma_start(tri3_unit[:, 0:S], tri_rows[:, LAST])
+        tri_t = [tri0[:], tri12[:, 0], tri12[:, 1], tri3_unit[:, 0:S]]
+        lod_t = keep.tile([P, TILES, U], F32, name="lod_all", tag="w1raw", align_bytes=64)
+        nc.sync.dma_start(lod_t[:], lod.rearrange("(p t) r -> p t r", t=TILES))
 
         def product_pass(bank, t, h, g):
             nc.tensor.matmul_mx(
                 bank[:],
                 lhsT=w1_codes[t][:, g, :].bitcast(FP4X4),
                 lhsT_scale=w1_planes[t][:, g, :],
-                rhs=xg[g][h][:].bitcast(FP8X4),
-                rhs_scale=sg[:, g, HALF * h : HALF * (h + 1)],
+                rhs=x_codes[g][h][:].bitcast(FP8X4),
+                rhs_scale=x_planes[:, g, BANK * h : BANK * (h + 1)],
                 start=(g == 0),
                 stop=(g == PASSES - 1),
             )
@@ -130,128 +140,163 @@ def tile_picked_yhashf_fade_p_kernel(
         y = {}
         for t in range(TILES):
             for h in range(2):
-                y[t, h] = psum.tile([P, HALF], F32, name=f"y{t}{h}", tag=f"bank{2 * t + h}")
-                for g in range(PASSES):
+                y[t, h] = psum.tile([P, BANK], F32, name=f"y{t}{h}", tag=f"bank{2 * t + h}")
+            for g in range(PASSES):
+                for h in range(2):
                     product_pass(y[t, h], t, h, g)
-        w2w = keep.tile([P, 2 * N], U8, name="w2w", tag="xg00", align_bytes=64)
-        w2s = keep.tile([P, N], U8, name="w2s", tag="xg01", align_bytes=64)
-        nc.gpsimd.memset(w2s[:].bitcast(I32), 0)
-        nc.sync.dma_start(w2w[:].bitcast(I32), w2_words[0].bitcast(I32))
-        for q in range(4):
-            nc.sync.dma_start(w2s[32 * q : 32 * q + 4, :].bitcast(I32), w2_scales[0, 4 * q : 4 * q + 4, :].bitcast(I32))
+        w2_codes = keep.tile([P, 2 * N], U8, name="w2w", tag="xg00", align_bytes=64)
+        w2_plane = keep.tile([P, N], U8, name="w2s", tag="xg01", align_bytes=64)
+        nc.gpsimd.memset(w2_plane[:].bitcast(I32), 0)
+        nc.sync.dma_start(w2_codes[:].bitcast(I32), w2_words[0].bitcast(I32))
+        for q in range(QUADS):
+            nc.sync.dma_start(
+                w2_plane[32 * q : 32 * q + 4, :].bitcast(I32), w2_scales[0, 4 * q : 4 * q + 4, :].bitcast(I32)
+            )
 
         hid = keep.tile([P, TILES, U], BF16, name="hid", align_bytes=64)
-        pw = [keep.tile([P, 3 * V], F32, name=f"pw{t}", align_bytes=64) for t in range(TILES - 1)]
-        first_turned = keep.tile([P, V], F32, name="first_turned", tag="first_turned", align_bytes=64)
-        rw = [keep.tile([P, (4 if t > 0 else 3) * V], F32, name=f"rw{t}", align_bytes=64) for t in range(TILES)]
-        pg = [keep.tile([P, V if t == 2 else U], F32, name=f"pg{t}", align_bytes=64) for t in range(TILES)]
-        rg = [keep.tile([P, U], F32, name=f"rg{t}", align_bytes=64) for t in range(TILES)]
+        totals = [keep.tile([P, (4 if t < FUSED else 3) * V], F32, name=f"pw{t}", align_bytes=64) for t in range(TILES)]
+        first_turned = keep.tile([P, V], F32, name="first_turned", align_bytes=64)
+        halves = [keep.tile([P, (4 if t == LAST else 3) * V], F32, name=f"rw{t}", align_bytes=64) for t in range(TILES)]
+        got_totals = {t: keep.tile([P, U], F32, name=f"pg{t}", align_bytes=64) for t in range(TILES) if t != FUSED}
+        got_halves = [keep.tile([P, U], F32, name=f"rg{t}", align_bytes=64) for t in range(TILES)]
+
+        def by_corner(t, h):
+            return y[t, h][:].rearrange("p (v d) -> p d v", d=D)
+
+        def upper_corners(t, h):
+            return totals[t][:, V : 3 * V].rearrange("p (e v) -> p e v", e=2)[:, :, CELLS * h : CELLS * (h + 1)]
 
         def copy_upper(t, h):
-            upper = pw[t][:, V : 3 * V].rearrange("p (e v) -> p e v", e=2)
-            cells = slice(CELLS * h, CELLS * (h + 1))
-            nc.scalar.activation(upper[:, :, cells], y[t, h][:].rearrange("p (v d) -> p d v", d=D)[:, 2:4], COPY, scale=0.5)
+            nc.scalar.activation(upper_corners(t, h), by_corner(t, h)[:, 2:4], COPY, scale=0.5)
 
-        def weigh(yw, t, h):
+        def weigh(weighted, t, h):
             cells = slice(CELLS * h, CELLS * (h + 1))
             nc.vector.tensor_tensor(
-                yw[:, :, cells, :].rearrange("p k v e -> p v k e"),
+                weighted[:, :, cells, :].rearrange("p k v e -> p v k e"),
                 y[t, h][:].rearrange("p (v k e) -> p v k e", k=2, e=2),
                 tri_t[t].rearrange("p (v k e) -> p v k e", k=2, e=2)[:, cells],
                 ALU.mult,
             )
 
-        def corners(t, yw):
-            run = keep.tile([P, 2, 2, V], F32, name=f"run{t}", tag="scratch", align_bytes=64)
-            upper = pw[t][:, V : 3 * V].rearrange("p (e v) -> p e v", e=2)
+        def corners(t, weighted):
+            pairs = keep.tile([P, 2, 2, V], F32, name=f"run{t}", tag="scratch", align_bytes=64)
             for h in range(2):
-                cells = slice(CELLS * h, CELLS * (h + 1))
-                weigh(yw, t, h)
+                if t > 0:
+                    weigh(weighted, t, h)
                 for c, op in enumerate((ALU.max, ALU.min)):
                     nc.vector.scalar_tensor_tensor(
-                        run[:, c, :, cells], y[t, h][:].rearrange("p (v d) -> p d v", d=D)[:, 0:2], 0.5, upper[:, :, cells], ALU.mult, op
+                        pairs[:, c, :, CELLS * h : CELLS * (h + 1)],
+                        by_corner(t, h)[:, 0:2],
+                        0.5,
+                        upper_corners(t, h),
+                        ALU.mult,
+                        op,
                     )
             for c, op in enumerate((ALU.max, ALU.min)):
-                nc.vector.tensor_tensor(rw[t][:, (1 + c) * V : (2 + c) * V], run[:, c, 0, :], run[:, c, 1, :], op)
-            eng = nc.gpsimd if t in RANGE_ON_GPSIMD else nc.vector
-            eng.tensor_tensor(rw[t][:, 0:V], rw[t][:, V : 2 * V], rw[t][:, 2 * V : 3 * V], ALU.subtract)
+                nc.vector.tensor_tensor(halves[t][:, (1 + c) * V : (2 + c) * V], pairs[:, c, 0, :], pairs[:, c, 1, :], op)
+            engine = nc.gpsimd if t < LAST else nc.vector
+            engine.tensor_tensor(halves[t][:, 0:V], halves[t][:, V : 2 * V], halves[t][:, 2 * V : 3 * V], ALU.subtract)
 
-        def tables(t, yw):
-            bank = psum.tile([P, HALF], F32, name=f"tp{t}", tag=f"bank{2 * t}")
-            halves = [slice(CELLS * h, CELLS * (h + 1)) for h in range(2)]
-            terms = [(cells, yw[:, k, cells, e]) for cells in halves for k in range(2) for e in range(2)]
-            terms = terms + [(cells, rw[t][:, cells]) for cells in halves]
+        def fetch(dst, window, first, last):
+            nc.scalar.activation(
+                dst[:, first:last], window[:].indirect(smp_t[:, first // PER_COLUMN : last // PER_COLUMN]), COPY
+            )
+
+        def tables(t, weighted):
+            bank = psum.tile([P, BANK], F32, name=f"tp{t}", tag=f"bank{2 * t}")
+            blocks = [slice(CELLS * h, CELLS * (h + 1)) for h in range(2)]
+            terms = [(cells, weighted[:, k, cells, e]) for cells in blocks for k in range(2) for e in range(2)]
+            terms = terms + [(cells, halves[t][:, cells]) for cells in blocks]
             for i, (cells, term) in enumerate(terms):
                 nc.tensor.matmul(
-                    bank[:, cells], lhsT=term, rhs=ident[:], is_transpose=True,
-                    start=(i == 0), stop=(i == len(terms) - 1),
+                    bank[:, cells],
+                    lhsT=term,
+                    rhs=ident[:],
+                    is_transpose=True,
+                    start=(i == 0),
+                    stop=(i == len(terms) - 1),
                 )
-            turned = rw[t][:, 3 * V :] if t > 0 else first_turned[:]
+            turned = [first_turned[:], totals[0][:, 3 * V :], totals[1][:, 3 * V :], halves[LAST][:, 3 * V :]][t]
+            if t < LAST:
+                fetch(got_halves[t], halves[t], 0, U)
             nc.scalar.copy(turned, bank[:, 0:V])
-            for h in range(2):
-                cells = slice(CELLS * h, CELLS * (h + 1))
+            for h, cells in enumerate(blocks):
                 nc.tensor.transpose(bank[:, V + CELLS * h : V + CELLS * (h + 1)], turned[:, cells], ident[:])
-            nc.scalar.activation(rg[t][:], rw[t][:].indirect(smp_t[:]), COPY)
-            nc.scalar.activation(pw[t][:, 0:V], bank[:, V : 2 * V], COPY, scale=unit_t[:, t : t + 1])
-            if t == 0:
-                pw.append(keep.tile([P, 3 * V], F32, name="pw3", tag="first_turned", align_bytes=64))
-                for h in range(2):
-                    copy_upper(TILES - 1, h)
-            for first, last in ([(0, U)], [(0, U)], [(0, V)], [(0, V), (V, U)])[t]:
-                nc.scalar.activation(pg[t][:, first:last], pw[t][:].indirect(smp_t[:, first // 16 : last // 16]), COPY)
+            if t == LAST:
+                fetch(got_halves[t], halves[t], 0, U)
+            elif t > 0:
+                fetch(got_totals[t - 1], totals[t - 1], 0, U)
+            nc.scalar.activation(totals[t][:, 0:V], bank[:, V : 2 * V], COPY, scale=unit_t[:, t : t + 1])
 
         def fade(faded, t, first, last):
-            sums = pw[t][:].indirect(smp_t[:, first // 16 : last // 16]) if (t, first) == (2, V) else pg[t][:, first:last]
-            nc.vector.tensor_tensor(faded[:, t, first:last], sums, lod_all[:, t, first:last], ALU.mult)
+            picked = totals[t][:].indirect(smp_t[:]) if t == FUSED else got_totals[t][:, first:last]
+            nc.vector.tensor_tensor(faded[:, t, first:last], picked, lod_t[:, t, first:last], ALU.mult)
 
         def finish(faded, t, first, last):
             nc.vector.scalar_tensor_tensor(
-                hid[:, t, first:last], rg[t][:, first:last], neg_unit[:, t : t + 1], faded[:, t, first:last], ALU.mult, ALU.add
+                hid[:, t, first:last],
+                got_halves[t][:, first:last],
+                neg_unit[:, t : t + 1],
+                faded[:, t, first:last],
+                ALU.mult,
+                ALU.add,
             )
 
-        for t in range(TILES - 1):
+        weighted = keep.tile([P, 2, V, 2], F32, name="yw0", tag="yw", bufs=2, align_bytes=64)
+        for h in range(2):
+            weigh(weighted, 0, h)
+        for t in range(TILES):
             for h in range(2):
                 copy_upper(t, h)
         nc.scalar.activation(neg_unit[:], unit_t, COPY, scale=-1.0)
         for t in range(TILES):
-            yw = keep.tile([P, 2, V, 2], F32, name=f"yw{t}", tag="yw", bufs=2, align_bytes=64)
-            corners(t, yw)
-            tables(t, yw)
+            if t > 0:
+                weighted = keep.tile([P, 2, V, 2], F32, name=f"yw{t}", tag="yw", bufs=2, align_bytes=64)
+            corners(t, weighted)
+            tables(t, weighted)
+        for h in range(2):
+            fetch(got_totals[LAST], totals[LAST], PART * h, PART * (h + 1))
+
         faded = keep.tile([P, TILES, U], F32, name="faded", tag="scratch", align_bytes=64)
         fade(faded, 0, 0, U)
-        fade(faded, 1, 0, U)
-        fade(faded, 2, V, U)
         finish(faded, 0, 0, U)
-        fade(faded, 2, 0, V)
-        finish(faded, 1, 0, U)
-        finish(faded, 2, 0, U)
+        for step in (fade, finish):
+            for t in (1, FUSED):
+                step(faded, t, 0, U)
         for step in (fade, finish):
             for h in range(2):
-                step(faded, 3, V * h, V * (h + 1))
+                step(faded, LAST, PART * h, PART * (h + 1))
 
-        woven = [keep.tile([P, V, TILES], BF16, name=f"woven{h}", align_bytes=64) for h in range(2)]
-        codes = [keep.tile([P, V], U32, name=f"codes{h}", align_bytes=64) for h in range(2)]
-        planes = [keep.tile([P, V], U8, name=f"planes{h}", align_bytes=64) for h in range(2)]
+        woven = [keep.tile([P, PART, TILES], BF16, name=f"woven{h}", align_bytes=64) for h in range(2)]
+        hid_codes = [keep.tile([P, PART], U32, name=f"codes{h}", align_bytes=64) for h in range(2)]
+        hid_planes = [keep.tile([P, PART], U8, name=f"planes{h}", align_bytes=64) for h in range(2)]
 
         def weave(copy, h, first, last):
             copy(
                 woven[h][:, first:last].rearrange("p (c i) t -> p c t i", i=4),
-                hid[:, :, V * h + first : V * h + last].rearrange("p t (c i) -> p c t i", i=4),
+                hid[:, :, PART * h + first : PART * h + last].rearrange("p t (c i) -> p c t i", i=4),
             )
 
         def decode(h):
-            nc.vector.quantize_mx(codes[h][:].bitcast(FP8X4), planes[h][:], woven[h][:].rearrange("p r t -> p (r t)"))
-            acc = psum.tile([P, V], F32, name=f"acc{h}", tag=f"bank{1 + 2 * h}")
-            nc.tensor.matmul_mx(
-                acc[:], lhsT=w2w[:].bitcast(FP4X4), lhsT_scale=w2s[:],
-                rhs=codes[h][:].bitcast(FP8X4), rhs_scale=planes[h][:], start=True, stop=True,
+            nc.vector.quantize_mx(
+                hid_codes[h][:].bitcast(FP8X4), hid_planes[h][:], woven[h][:].rearrange("p r t -> p (r t)")
             )
-            res = keep.tile([P, V], F32, name=f"res{h}", align_bytes=64)
-            nc.scalar.copy(res[:], acc[:])
-            nc.scalar.dma_start(out[:, V * h : V * (h + 1)], res[:])
+            acc = psum.tile([P, PART], F32, name=f"acc{h}", tag=f"bank{1 + 2 * h}")
+            nc.tensor.matmul_mx(
+                acc[:],
+                lhsT=w2_codes[:].bitcast(FP4X4),
+                lhsT_scale=w2_plane[:],
+                rhs=hid_codes[h][:].bitcast(FP8X4),
+                rhs_scale=hid_planes[h][:],
+                start=True,
+                stop=True,
+            )
+            result = keep.tile([P, PART], F32, name=f"res{h}", align_bytes=64)
+            nc.scalar.copy(result[:], acc[:])
+            nc.scalar.dma_start(out[:, PART * h : PART * (h + 1)], result[:])
 
-        weave(nc.scalar.copy, 0, 0, V // 2)
-        weave(nc.vector.tensor_copy, 0, V // 2, V)
-        weave(nc.vector.tensor_copy, 1, 0, V)
+        weave(nc.scalar.copy, 0, 0, PART // 2)
+        weave(nc.vector.tensor_copy, 0, PART // 2, PART)
+        weave(nc.vector.tensor_copy, 1, 0, PART)
         decode(0)
         decode(1)

from contextlib import ExitStack

import concourse.mybir as mybir
from concourse.masks import make_identity

K, T, S, D, N, H, V, U = 1024, 2048, 1024, 4, 128, 512, 256, 512
FLOPS = 2 * K * H * S + 2 * H * N * U

F32 = mybir.dt.float32
BF16 = mybir.dt.bfloat16
I32 = mybir.dt.int32
U32 = mybir.dt.uint32
U16 = mybir.dt.uint16
U8 = mybir.dt.uint8
FP8X4 = mybir.dt.float8_e4m3fn_x4
FP4X4 = mybir.dt.float4_e2m1fn_x4
ALU = mybir.AluOpType
COPY = mybir.ActivationFunctionType.Copy

P = 128
PASSES = K // 512
TILES = H // P
LAST = TILES - 1
FUSED = 2
QUADS = 4
BANK = 512
CELLS = BANK // D
PART = U // 2
PER_COLUMN = 16
PAD = 16


def tile_picked_yhashf_fade_p_kernel(
    tc, x_words, x_scales, w1_words, w1_scales, tri, lod, unit, w2_words, w2_scales, offs, smp, out
):
    nc = tc.nc
    with ExitStack() as ctx:
        keep = ctx.enter_context(tc.tile_pool(name="keep", bufs=1))
        psum = ctx.enter_context(tc.psum_pool(name="psum", bufs=1))

        offs_t = keep.tile([P, S // PER_COLUMN], U16, name="offs_t")
        smp_t = keep.tile([P, U // PER_COLUMN], U16, name="smp_t")
        x_table = [keep.tile([P, T], U32, name=f"xw{g}", tag=f"xw{g}", align_bytes=64) for g in range(PASSES)]
        scale_table = keep.tile([P, T], U8, name="xs", tag="xs", align_bytes=64)
        w1_raw = keep.tile([P, PASSES, 2 * H], U8, name="w1raw", tag="w1raw", align_bytes=64)
        w1_raw_planes = keep.tile([P, PASSES, H], U8, name="w1sraw", tag="w1sraw", align_bytes=64)
        early = keep.tile([P, 2 * PASSES * 3 * P], U8, name="early", align_bytes=64)
        picked_rows = keep.tile([P, S], U8, name="sg0", tag="sg0", align_bytes=64)
        x_planes = keep.tile([P, PASSES, S], U8, name="sg", align_bytes=64)
        x_codes = [
            [keep.tile([P, BANK], U32, name=f"xg{g}{h}", tag=f"xg{g}{h}", align_bytes=64) for h in range(2)]
            for g in range(PASSES)
        ]
        neg_unit = keep.tile([P, TILES], F32, name="neg_unit")
        ident = keep.tile([P, P], F32, name="ident", align_bytes=64)

        nc.vector.memset(w1_raw_planes[:].rearrange("p g c -> p (g c)").bitcast(I32), 0)
        nc.vector.memset(scale_table[64:128, :].bitcast(I32), 0)
        nc.gpsimd.memset(scale_table[32:64, :].bitcast(I32), 0)
        nc.gpsimd.memset(x_planes[:].rearrange("p g c -> p (g c)").bitcast(I32), 0)
        make_identity(nc, ident[:])

        def load_words(g):
            nc.sync.dma_start(x_table[g][:].bitcast(I32), x_words[g].rearrange("p n j -> p (n j)").bitcast(I32))

        nc.sync.dma_start(scale_table[0:32, :].bitcast(I32), x_scales.rearrange("g q c -> q g c").bitcast(I32))
        nc.sync.dma_start(offs_t[:], offs)
        nc.sync.dma_start(w1_raw[:].bitcast(I32), w1_words.rearrange("g p b -> p g b").bitcast(I32))
        load_words(0)
        for q in range(QUADS):
            nc.sync.dma_start(
                w1_raw_planes[32 * q : 32 * q + 4].bitcast(I32),
                w1_scales[:, 4 * q : 4 * q + 4, :].rearrange("g r c -> r g c").bitcast(I32),
            )
        load_words(1)
        nc.sync.dma_start(smp_t[:], smp)

        nc.vector.tensor_copy(picked_rows[:], scale_table[:].indirect(offs_t[:]))
        for q in range(QUADS):
            nc.sync.dma_start(
                x_planes[32 * q : 32 * q + 4].rearrange("p g c -> p (g c)").bitcast(I32),
                picked_rows[8 * q : 8 * q + 8, :].bitcast(I32),
            )

        def gather_words(g, h):
            columns = BANK // PER_COLUMN
            nc.vector.tensor_copy(x_codes[g][h][:], x_table[g][:].indirect(offs_t[:, columns * h : columns * (h + 1)]))

        def dealt_views(tile):
            words = tile[:, 0 : 2 * PASSES * 2 * P].rearrange("p (t g b) -> p t g b", t=2, g=PASSES)
            scales = tile[:, 2 * PASSES * 2 * P :].rearrange("p (t g m) -> p t g m", t=2, g=PASSES)
            return words, scales

        raw_scales = w1_raw_planes[:].rearrange("p g (m t) -> p t g m", t=TILES)
        words_01, scales_01 = dealt_views(early)
        nc.vector.tensor_copy(
            words_01.bitcast(U16), w1_raw[:].bitcast(U16).rearrange("p g (m t) -> p t g m", t=TILES)[:, 0:2]
        )
        gather_words(0, 0)
        nc.vector.tensor_copy(scales_01[:, 0], raw_scales[:, 0])
        gather_words(0, 1)
        gather_words(1, 0)
        gather_words(1, 1)
        late = keep.tile([P, 2 * PASSES * 3 * P + PASSES * P], U8, name="late", tag="xw1", align_bytes=64)
        words_23, scales_23 = dealt_views(late[:, 0 : 2 * PASSES * 3 * P])
        scales_1 = late[:, 2 * PASSES * 3 * P :].rearrange("p (g m) -> p g m", g=PASSES)
        nc.vector.tensor_copy(scales_1, raw_scales[:, 1])
        raw_words = w1_raw[:].rearrange("p g (m t b) -> p t g m b", t=TILES, b=2)
        for t in range(2):
            nc.gpsimd.tensor_copy(words_23[:, t].rearrange("p g (m b) -> p g m b", b=2), raw_words[:, 2 + t])
            nc.gpsimd.tensor_copy(scales_23[:, t], raw_scales[:, 2 + t])
        w1_codes = [words_01[:, 0], words_01[:, 1], words_23[:, 0], words_23[:, 1]]
        w1_planes = [scales_01[:, 0], scales_1, scales_23[:, 0], scales_23[:, 1]]

        tri_rows = tri.rearrange("(p t) j -> p t j", t=TILES)
        tri0 = keep.tile([P, S], F32, name="tri0", tag="xs", align_bytes=64)
        nc.sync.dma_start(tri0[:], tri_rows[:, 0])
        tri12 = keep.tile([P, 2, S], F32, name="tri12", tag="xw0", align_bytes=64)
        for t in range(2):
            nc.sync.dma_start(tri12[:, t], tri_rows[:, 1 + t])
        tri3_unit = keep.tile([P, S + PAD], F32, name="tri3", tag="sg0", align_bytes=64)
        unit_t = tri3_unit[:, S : S + TILES]
        nc.sync.dma_start(unit_t, unit.rearrange("(p t) o -> p (t o)", t=TILES))
        nc.sync.dma_start(tri3_unit[:, 0:S], tri_rows[:, LAST])
        tri_t = [tri0[:], tri12[:, 0], tri12[:, 1], tri3_unit[:, 0:S]]
        lod_t = keep.tile([P, TILES, U], F32, name="lod_all", tag="w1raw", align_bytes=64)
        nc.sync.dma_start(lod_t[:], lod.rearrange("(p t) r -> p t r", t=TILES))

        def product_pass(bank, t, h, g):
            nc.tensor.matmul_mx(
                bank[:],
                lhsT=w1_codes[t][:, g, :].bitcast(FP4X4),
                lhsT_scale=w1_planes[t][:, g, :],
                rhs=x_codes[g][h][:].bitcast(FP8X4),
                rhs_scale=x_planes[:, g, BANK * h : BANK * (h + 1)],
                start=(g == 0),
                stop=(g == PASSES - 1),
            )

        y = {}
        for t in range(TILES):
            for h in range(2):
                y[t, h] = psum.tile([P, BANK], F32, name=f"y{t}{h}", tag=f"bank{2 * t + h}")
            for g in range(PASSES):
                for h in range(2):
                    product_pass(y[t, h], t, h, g)
        w2_codes = keep.tile([P, 2 * N], U8, name="w2w", tag="xg00", align_bytes=64)
        w2_plane = keep.tile([P, N], U8, name="w2s", tag="xg01", align_bytes=64)
        nc.gpsimd.memset(w2_plane[:].bitcast(I32), 0)
        nc.sync.dma_start(w2_codes[:].bitcast(I32), w2_words[0].bitcast(I32))
        for q in range(QUADS):
            nc.sync.dma_start(
                w2_plane[32 * q : 32 * q + 4, :].bitcast(I32), w2_scales[0, 4 * q : 4 * q + 4, :].bitcast(I32)
            )

        hid = keep.tile([P, TILES, U], BF16, name="hid", align_bytes=64)
        totals = [keep.tile([P, (4 if t < FUSED else 3) * V], F32, name=f"pw{t}", align_bytes=64) for t in range(TILES)]
        first_turned = keep.tile([P, V], F32, name="first_turned", align_bytes=64)
        halves = [keep.tile([P, (4 if t == LAST else 3) * V], F32, name=f"rw{t}", align_bytes=64) for t in range(TILES)]
        got_totals = {t: keep.tile([P, U], F32, name=f"pg{t}", align_bytes=64) for t in range(TILES) if t != FUSED}
        got_halves = [keep.tile([P, U], F32, name=f"rg{t}", align_bytes=64) for t in range(TILES)]

        def by_corner(t, h):
            return y[t, h][:].rearrange("p (v d) -> p d v", d=D)

        def upper_corners(t, h):
            return totals[t][:, V : 3 * V].rearrange("p (e v) -> p e v", e=2)[:, :, CELLS * h : CELLS * (h + 1)]

        def copy_upper(t, h):
            nc.scalar.activation(upper_corners(t, h), by_corner(t, h)[:, 2:4], COPY, scale=0.5)

        def weigh(weighted, t, h):
            cells = slice(CELLS * h, CELLS * (h + 1))
            nc.vector.tensor_tensor(
                weighted[:, :, cells, :].rearrange("p k v e -> p v k e"),
                y[t, h][:].rearrange("p (v k e) -> p v k e", k=2, e=2),
                tri_t[t].rearrange("p (v k e) -> p v k e", k=2, e=2)[:, cells],
                ALU.mult,
            )

        def corners(t, weighted):
            pairs = keep.tile([P, 2, 2, V], F32, name=f"run{t}", tag="scratch", align_bytes=64)
            for h in range(2):
                if t > 0:
                    weigh(weighted, t, h)
                for c, op in enumerate((ALU.max, ALU.min)):
                    nc.vector.scalar_tensor_tensor(
                        pairs[:, c, :, CELLS * h : CELLS * (h + 1)],
                        by_corner(t, h)[:, 0:2],
                        0.5,
                        upper_corners(t, h),
                        ALU.mult,
                        op,
                    )
            for c, op in enumerate((ALU.max, ALU.min)):
                nc.vector.tensor_tensor(halves[t][:, (1 + c) * V : (2 + c) * V], pairs[:, c, 0, :], pairs[:, c, 1, :], op)
            engine = nc.gpsimd if t < LAST else nc.vector
            engine.tensor_tensor(halves[t][:, 0:V], halves[t][:, V : 2 * V], halves[t][:, 2 * V : 3 * V], ALU.subtract)

        def fetch(dst, window, first, last):
            nc.scalar.activation(
                dst[:, first:last], window[:].indirect(smp_t[:, first // PER_COLUMN : last // PER_COLUMN]), COPY
            )

        def tables(t, weighted):
            bank = psum.tile([P, BANK], F32, name=f"tp{t}", tag=f"bank{2 * t}")
            blocks = [slice(CELLS * h, CELLS * (h + 1)) for h in range(2)]
            terms = [(cells, weighted[:, k, cells, e]) for cells in blocks for k in range(2) for e in range(2)]
            terms = terms + [(cells, halves[t][:, cells]) for cells in blocks]
            for i, (cells, term) in enumerate(terms):
                nc.tensor.matmul(
                    bank[:, cells],
                    lhsT=term,
                    rhs=ident[:],
                    is_transpose=True,
                    start=(i == 0),
                    stop=(i == len(terms) - 1),
                )
            turned = [first_turned[:], totals[0][:, 3 * V :], totals[1][:, 3 * V :], halves[LAST][:, 3 * V :]][t]
            if t < LAST:
                fetch(got_halves[t], halves[t], 0, U)
            nc.scalar.copy(turned, bank[:, 0:V])
            for h, cells in enumerate(blocks):
                nc.tensor.transpose(bank[:, V + CELLS * h : V + CELLS * (h + 1)], turned[:, cells], ident[:])
            if t == LAST:
                fetch(got_halves[t], halves[t], 0, U)
            elif t > 0:
                fetch(got_totals[t - 1], totals[t - 1], 0, U)
            nc.scalar.activation(totals[t][:, 0:V], bank[:, V : 2 * V], COPY, scale=unit_t[:, t : t + 1])

        def fade(faded, t, first, last):
            picked = totals[t][:].indirect(smp_t[:]) if t == FUSED else got_totals[t][:, first:last]
            nc.vector.tensor_tensor(faded[:, t, first:last], picked, lod_t[:, t, first:last], ALU.mult)

        def finish(faded, t, first, last):
            nc.vector.scalar_tensor_tensor(
                hid[:, t, first:last],
                got_halves[t][:, first:last],
                neg_unit[:, t : t + 1],
                faded[:, t, first:last],
                ALU.mult,
                ALU.add,
            )

        weighted = keep.tile([P, 2, V, 2], F32, name="yw0", tag="yw", bufs=2, align_bytes=64)
        for h in range(2):
            weigh(weighted, 0, h)
        for t in range(TILES):
            for h in range(2):
                copy_upper(t, h)
        nc.scalar.activation(neg_unit[:], unit_t, COPY, scale=-1.0)
        for t in range(TILES):
            if t > 0:
                weighted = keep.tile([P, 2, V, 2], F32, name=f"yw{t}", tag="yw", bufs=2, align_bytes=64)
            corners(t, weighted)
            tables(t, weighted)
        for h in range(2):
            fetch(got_totals[LAST], totals[LAST], PART * h, PART * (h + 1))

        faded = keep.tile([P, TILES, U], F32, name="faded", tag="scratch", align_bytes=64)
        fade(faded, 0, 0, U)
        finish(faded, 0, 0, U)
        for step in (fade, finish):
            for t in (1, FUSED):
                step(faded, t, 0, U)
        for step in (fade, finish):
            for h in range(2):
                step(faded, LAST, PART * h, PART * (h + 1))

        woven = [keep.tile([P, PART, TILES], BF16, name=f"woven{h}", align_bytes=64) for h in range(2)]
        hid_codes = [keep.tile([P, PART], U32, name=f"codes{h}", align_bytes=64) for h in range(2)]
        hid_planes = [keep.tile([P, PART], U8, name=f"planes{h}", align_bytes=64) for h in range(2)]

        def weave(copy, h, first, last):
            copy(
                woven[h][:, first:last].rearrange("p (c i) t -> p c t i", i=4),
                hid[:, :, PART * h + first : PART * h + last].rearrange("p t (c i) -> p c t i", i=4),
            )

        def decode(h):
            nc.vector.quantize_mx(
                hid_codes[h][:].bitcast(FP8X4), hid_planes[h][:], woven[h][:].rearrange("p r t -> p (r t)")
            )
            acc = psum.tile([P, PART], F32, name=f"acc{h}", tag=f"bank{1 + 2 * h}")
            nc.tensor.matmul_mx(
                acc[:],
                lhsT=w2_codes[:].bitcast(FP4X4),
                lhsT_scale=w2_plane[:],
                rhs=hid_codes[h][:].bitcast(FP8X4),
                rhs_scale=hid_planes[h][:],
                start=True,
                stop=True,
            )
            result = keep.tile([P, PART], F32, name=f"res{h}", align_bytes=64)
            nc.scalar.copy(result[:], acc[:])
            nc.scalar.dma_start(out[:, PART * h : PART * (h + 1)], result[:])

        weave(nc.scalar.copy, 0, 0, PART // 2)
        weave(nc.vector.tensor_copy, 0, PART // 2, PART)
        weave(nc.vector.tensor_copy, 1, 0, PART)
        decode(0)
        decode(1)
